import numpy as np, ml_dtypes
CORES = [113,118,241,246]
N = 4
BF = ml_dtypes.bfloat16
W, P, L, SH, RO = 4096, 192, 8, 5, 3
def parts(rng):
    return (rng.integers(0, 256, (N, 8, 16, W)), rng.integers(0, W, (N, 8, 16, P)), rng.integers(0, W, (N, 8, 16, P)),
            rng.integers(500, 1300, (N, 8, 16)), rng.integers(30, 100, (N, 8, 16)))
def pack(x, r, m, t, e):
    return {"flood": np.ascontiguousarray(x.reshape(N, 128, W)).astype(np.float32).astype(BF), "riv": np.ascontiguousarray(r.reshape(N, 128, P)).astype(np.int32),
            "bord": np.ascontiguousarray(m.reshape(N, 128, P)).astype(np.int32), "th": t.reshape(N, 128, 1).astype(np.int32), "eps": e.reshape(N, 128, 1).astype(np.int32)}
def setup_inputs(rng):
    return pack(*parts(rng))
def setup_inputs_spread(rng):
    x = np.minimum((np.exp2(3 + 5.5 * rng.random((N, 8, 1, W))) * rng.random((N, 8, 16, W))).astype(np.int64), 255)
    r = (W * rng.random((N, 8, 16, P)) ** 3).astype(np.int64); m = W - 1 - (W * rng.random((N, 8, 16, P)) ** 3).astype(np.int64)
    t = np.minimum(np.exp2(7 + 5 * rng.random((N, 8, 16))).astype(np.int64), 4080); e = np.minimum(np.exp2(8 * rng.random((N, 8, 16))).astype(np.int64) - 1, 255)
    return pack(x, r, m, t, e)
def setup_inputs_ends(rng):
    x = 255 * rng.integers(0, 2, (N, 8, 16, W)); pure = 255 * rng.integers(0, 2, (N, 8, 1, W))
    kind = rng.random((N, 8)) < 0.4; kind[:, 7] = True
    x = np.where(kind[:, :, None, None], pure, x)
    k2 = (((W - 1) * (W - 1) >> SH) + 38 * (W - 1)) & (W - 1)
    x[:, 7, :, 0] = 0
    for c in (W - 1, W - 37, k2): x[:, 7, :, c] = 255
    r = (W - 1) * rng.integers(0, 2, (N, 8, 16, P)); m = (W - 1) * rng.integers(0, 2, (N, 8, 16, P))
    t = 4080 * rng.integers(0, 2, (N, 8, 16)); t[:, :, 2] = 0; t[:, :, 5] = 4080
    e = np.zeros((N, 8, 16), np.int64)
    for q in range(N):
        for g in range(8):
            n = int(rng.choice(np.array([0, 7, 8, 8, 9, 9, 16])))
            if g == 7: n = 8 + q % 2
            e[q, g, rng.permutation(16)[:n]] = 255
    for p in (1, 8, 15):
        r[:, 7, p] = np.where((np.arange(P) // L) % 2 == 0, W - 1, 0); m[:, 7, p] = W - 1; t[:, 7, p] = 4080
    for p in (0, 3, 14):
        r[:, 7, p] = W - 1; r[:, 7, p, P - 1] = 0; m[:, 7, p] = W - 1
    t[:, 7, 0] = 0; t[:, 7, 14] = 0
    r[:, 7, 10] = ((W - 1) * (np.arange(N) % 2))[:, None]; m[:, 7, 10] = W - 1; t[:, 7, 10] = 4080
    return pack(x, r, m, t, e)
def setup_inputs_corners(rng):
    x, r, m, t, e = parts(rng)
    r = np.argsort(rng.random((N, 8, 16, W)), axis=-1)[..., :P]; r = np.ascontiguousarray(r)
    kd = rng.integers(0, 7, (N, 8, 16)); kd[:, 0] = 6; kd[0::2, 3] = 0; kd[1::2, 3] = 6; kd[:, 7, 14] = 5; kd[:, 7, 15] = 2
    r[..., L] = np.where((kd == 1) | (kd == 3), r[..., 0], r[..., L])
    r[..., P - 1] = np.where((kd == 2) | (kd == 3), r[..., P - 1 - L], r[..., P - 1])
    m = np.where(rng.random((N, 8, 16, P)) < 0.3, r, m); e = np.zeros((N, 8, 16), np.int64)
    for q in range(N):
        for g in range(8):
            k = 8 if g in (0, 7) else int(rng.choice(np.array([7, 8, 8, 9]))); o = rng.permutation(16)
            x[q, g, o[:k]] = rng.integers(0, 256, (k, 1))
            n = max(0, 9 - k - int(rng.integers(0, 2))); e[q, g, o[k:k + n]] = 255
            v = x[q, g][:, r[q, g]]; s = np.min(np.add.reduce(np.abs(v[..., :P - L] - v[..., L:]), axis=0), axis=-1); c = kd[q, g]
            t[q, g] = np.where(c == 0, 0, np.where(c < 4, 1, np.where(c == 4, s, np.where(c == 5, np.minimum(s + 1, 4080), 4080))))
    return pack(x, r, m, t, e)
def setup_inputs_ties(rng):
    x = rng.integers(0, 4, (N, 8, 16, W)); r, m = rng.integers(0, W, (2, N, 8, 16, P))
    w = rng.integers(0, W, (N, 4, 1, 12)); w[..., 0] = 0; w[..., 11] = W - 1
    r[:, 1::2] = np.take_along_axis(np.broadcast_to(w, (N, 4, 16, 12)), rng.integers(0, 12, (N, 4, 16, P)), -1)
    m[:, ::2] = np.where(rng.random((N, 4, 16, P)) < 0.5, r[:, ::2], m[:, ::2])
    return pack(x, r, m, rng.integers(0, 18, (N, 8, 16)), rng.integers(0, 3, (N, 8, 16)))
def setup_inputs_far(rng):
    k = W // 16; n = W - 2 * k; pos = np.argsort(rng.random((N, 8, W)), axis=-1); o = np.argsort(pos, axis=-1)
    share = np.where(np.arange(8) % 2 == 0, 0.5, rng.choice(np.array([0.2, 0.8]), (N, 8)))
    hn = (share * n).astype(np.int64)[..., None]; high = (pos >= k) & (pos < 2 * k + hn)
    x = np.where((pos < 2 * k)[:, :, None], 0, rng.integers(0, 8, (N, 8, 16, W))); x = np.where(high[:, :, None], 255 - x, x)
    c = rng.integers(0, 2, (N, 8, 16, P)); c[:, :, ::2] = (np.arange(P) // L + rng.integers(0, 2, (N, 8, 8, 1))) % 2; c[:, :, 1::4, P - 1] = 0
    u = rng.random((N, 8, 16, P)); hn = hn[..., None]; odd = (np.arange(16) % 2 == 1)[:, None]
    mixed = np.where(c == 1, 2 * k + (u * hn).astype(np.int64), 2 * k + hn + (u * (n - hn)).astype(np.int64))
    i = np.where(odd, c * k + (u * k).astype(np.int64), mixed)
    r = np.take_along_axis(o, i.reshape(N, 8, -1), -1).reshape(N, 8, 16, P)
    i = (1 - c) * k + rng.integers(0, k, (N, 8, 16, P)); far = np.take_along_axis(o, i.reshape(N, 8, -1), -1).reshape(N, 8, 16, P)
    m = np.where(odd & (rng.random((N, 8, 16, P)) < 0.25), far, rng.integers(0, W, (N, 8, 16, P))); m[:, :, 1::4, P - 1] = far[:, :, 1::4, P - 1]
    t = rng.integers(3925, 3976, (N, 8, 16)); t[:, :, ::4] = 3929 + 4 * rng.integers(0, 12, (N, 8, 4)); t[:, :, 1::4] = 0; t[:, :, 3::4] = rng.integers(3900, 4080, (N, 8, 4))
    e = np.where(np.argsort(rng.random((N, 8, 16)), axis=-1) < 12, 254, rng.integers(247, 255, (N, 8, 16)))
    return pack(x, r, m, t, e)
def check_inputs(d):
    bad = []
    for k, lo, hi in (("flood", 0, 255), ("riv", 0, W - 1), ("bord", 0, W - 1), ("th", 0, 4080), ("eps", 0, 255)):
        v = np.asarray(d[k]).astype(np.float64)
        if not (np.all(v >= lo) and np.all(v <= hi)): bad.append("range of " + k)
        elif not np.all(v == np.floor(v)): bad.append("whole numbers in " + k)
    return bad
def columns(x, names):
    return np.take(x, names + W * np.arange(8)[:, None, None], axis=0)
def total(v):
    return np.add.reduce(v, axis=-1, dtype=np.int16)
def reference(flood, riv, bord, th, eps):
    R = riv.astype(np.int64).reshape(N, 8, 16, P); M = bord.astype(np.int64).reshape(N, 8, 16, P); A = np.zeros((N, 8, 16), np.int64)
    T = th.astype(np.int64).reshape(N, 8, 16); E = eps.astype(np.int16).reshape(N, 8, 1, 1, 16)
    X = [np.ascontiguousarray(a.astype(np.float32).astype(np.int16).reshape(8, 16, W).transpose(0, 2, 1)).reshape(8 * W, 16) for a in flood]
    place = np.arange(P)
    for t in range(RO):
        first = np.zeros((N, 8, 16), np.int64); loops = np.zeros((N, 8, 16, L), np.int64)
        for q in range(N):
            r, m = R[q], M[q]; h = r[..., :P - 1]; x = columns(X[q], r); nxt = x[:, :, 1:]; now = np.abs(x[:, :, :P - 1] - nxt)
            before = np.concatenate([r[..., :1], r[..., :P - 2]], axis=-1)
            cand = np.stack([((h * a >> SH) + 37 * h + a + 77 * t) & (W - 1) for a in (before, r[..., 1:], m[..., :P - 1], m[..., 1:])] + [m[..., :P - 1]])
            score = np.stack([total(np.abs(columns(X[q], c) - nxt)) for c in cand])
            best = np.take_along_axis(cand, np.argmin(score, axis=0)[None], 0)[0]
            near = total((np.abs(columns(X[q], best) - nxt) < now).astype(np.int16))
            R[q, :, :, :P - 1] = np.where(near >= 9, best, h)
            x = columns(X[q], R[q]); ok = total(np.abs(x[:, :, :P - L] - x[:, :, L:])) < (T[q] + 16 * A[q])[..., None]
            first[q] = np.where(np.any(ok, axis=-1), np.argmax(ok, axis=-1), P)
            loops[q] = np.take_along_axis(R[q], np.minimum(first[q] + 1, P - L)[..., None] + np.arange(L), -1)
        for q in range(N):
            src = (q - 1 - t % (N - 1)) % N
            lp = np.where((first[src] < P)[..., None], loops[src], loops[q])
            R[q] = np.take_along_axis(np.concatenate([R[q], lp], axis=-1), place + L * (place > first[q][..., None]), -1)
            A[q] = A[q] + (first[q] < P)
            near = total((np.abs(columns(X[q], R[q]) - columns(X[q], M[q])) <= E[q]).astype(np.int16))
            M[q] = np.where(near >= 9, R[q], M[q])
    return {"yr": R.reshape(N, 128, P).astype(np.float32), "ym": M.reshape(N, 128, P).astype(np.float32), "ya": A.reshape(N, 128, 1).astype(np.float32)}

@@ -1,0 +1,540 @@
+import numpy as np
+from concourse.mybir import AluOpType as ALU, AxisListType, ActivationFunctionType as ACT
+
+W, P, L, RO = 4096, 192, 8, 3
+H = 262144
+CH = [[40, 80, 136, 192], [48, 96, 136, 192], [64, 88, 128, 192]]
+BF, F32, I32, U16 = "bfloat16", "float32", "int32", "uint16"
+
+SCRATCH = {
+    "FL": ("sbuf", [128, W], BF),
+    "ONE": ("sbuf", [128, 144], BF), "Z": ("sbuf", [128, 144], BF), "ZK": ("sbuf", [128, 144], BF), "ZH": ("sbuf", [128, 144], BF),
+    "WI": ("sbuf", [128, 144], I32), "WJ": ("sbuf", [128, 320], I32), "WK": ("sbuf", [128, 128], I32),
+    "IP": ("sbuf", [128, 128], BF), "IN": ("sbuf", [128, 128], BF), "IK": ("sbuf", [128, 128], BF), "IF": ("sbuf", [128, 128], F32),
+    "KL": ("sbuf", [128, 128], BF), "KR": ("sbuf", [128, 320], BF), "CP": ("sbuf", [128, 64], BF), "CN": ("sbuf", [128, 64], BF), "CC": ("sbuf", [128, 320], BF),
+    "RSK": ("sbuf", [128, 320], F32), "RST": ("sbuf", [128, 320], F32), "DM": ("sbuf", [128, 128], F32), "K8": ("sbuf", [128, 8], F32),
+    "thi": ("sbuf", [128, 1], I32), "epi": ("sbuf", [128, 1], I32), "EPF": ("sbuf", [128, 1], F32),
+    "OUTR": ("sbuf", [128, P], F32), "OUTM": ("sbuf", [128, P], F32), "OUTA": ("sbuf", [128, 1], F32),
+    "LG": ("sbuf", [128, 128], F32), "LM": ("sbuf", [128, 128], F32), "L64": ("sbuf", [128, 64], F32), "L32": ("sbuf", [128, 32], F32),
+    "L16": ("sbuf", [128, 16], F32), "LO": ("sbuf", [128, 8], F32), "SPM": ("sbuf", [128, 1], F32), "OFF": ("sbuf", [128, 8], U16),
+    "NPM": ("sbuf", [128, 1], F32), "RTK": ("sbuf", [128, 8], F32), "BASE": ("sbuf", [128, 8], F32),
+    "SA": ("psum", [128, 1024], F32), "SB": ("psum", [128, 1024], F32), "KY": ("psum", [128, 512], F32),
+    "TB": ("psum", [128, 512], F32), "MS": ("psum", [128, 512], F32), "RV": ("psum", [128, 512], F32),
+}
+for _m in range(4):
+    SCRATCH["IM%d" % _m] = ("sbuf", [128, 128], BF)
+for _t in range(RO):
+    SCRATCH["SND%d" % _t] = ("sbuf", [128, 8], F32)
+    SCRATCH["LAND%d" % _t] = ("sbuf", [128, 8], F32)
+for _t in range(RO + 1):
+    SCRATCH["THR%d" % _t] = ("sbuf", [128, 1], F32)
+for _k in range(2):
+    for _n, _w, _d in (("XR", 3088, BF), ("XM", 3072, BF), ("ABS", 5120, BF), ("NOW", 1024, BF), ("FB", 1024, BF), ("NA", 1024, BF),
+                       ("MX", 1024, BF), ("MB", 1024, BF), ("QF", 256, F32), ("QI", 256, I32), ("CI", 256, I32), ("CU", 256, U16),
+                       ("TS", 320, F32), ("KS", 320, F32), ("KI", 64, I32), ("KO", 64, I32), ("KU", 64, U16), ("NI", 64, I32),
+                       ("NB", 64, BF), ("DS", 320, F32), ("OK", 64, BF), ("RI", P, I32), ("RU", P, U16), ("RA", 208, F32),
+                       ("MI", P, I32), ("MU", P, U16), ("MA", 208, F32), ("MH", P, F32), ("PI", P, I32), ("PU", P, U16),
+                       ("PF", 200, F32), ("PM", 208, BF)):
+        SCRATCH["%s%d" % (_n, _k)] = ("sbuf", [128, _w], _d)
+SCRATCH["XP"] = ("sbuf", [128, 3072], BF)
+SCRATCH["XD"] = ("sbuf", [128, 4096], BF)
+
+for _k in range(4):
+    SCRATCH["TI%d" % _k] = ("sbuf", [128, 64], I32)
+QSEM = {"v": "cv", "s": "cs", "t": "ct", "g": "cg"}
+SEMAPHORES = ["cv", "cs", "ct", "cg", "sent", "arr0", "arr1", "arr2"] + ["ld%d" % k for k in range(6)] + ["st%d" % k for k in range(8)]
+CYC = 0.83e-3 * 1.25
+GAM = 1.5
+WAKE = 0.08
+SLACK, NOISE, SEED = 0.0, 0.0, 0
+PLAIN = [()]
+PEF = 0.5
+AGE = 0.0
+GQ = [{"x": "vs"}.get(c, c) for c in "xsvxssssssssssssxssssxsxssssssssssxvsssssvxsvsssss"]
+
+
+def plan(core, T, topo):
+    ops = []
+    rank = T.rank_of(core)
+
+    def add(q, cost, reads, writes, fn, sem=None, inc=1, after=(), free=False):
+        ops.append({"q": q, "cost": cost, "r": reads, "w": writes, "fn": fn, "sem": sem, "inc": inc, "after": list(after),
+                    "free": free})
+        return len(ops) - 1
+
+    def ap(x):
+        n, a, b = x[0], x[1], x[2]
+        return T[n][:, a:b] if len(x) == 3 else T[n][:, a:b:x[3]]
+
+    def vc(n, f=1.0):
+        return max(64, n * f) * CYC + 0.02
+
+    def copy(out, in_, f=1.0):
+        add("v", vc((out[2] - out[1]) // (out[3] if len(out) > 3 else 1), f), [in_], [out], lambda e: e.tensor_copy(ap(out), ap(in_)))
+
+    def ts(out, in_, s1, op0, s2=None, op1=None, f=1.0, n=None):
+        rd = [in_] + [s for s in (s1, s2) if not isinstance(s, (int, float)) and s is not None]
+        v1 = s1 if isinstance(s1, (int, float)) else ap(s1)
+        v2 = s2 if s2 is None or isinstance(s2, (int, float)) else ap(s2)
+        if op1 is None:
+            add("v", vc(n or in_[2] - in_[1], f), rd, [out], lambda e: e.tensor_scalar(ap(out), ap(in_), v1, None, op0))
+        else:
+            add("v", vc(n or in_[2] - in_[1], f), rd, [out], lambda e: e.tensor_scalar(ap(out), ap(in_), v1, v2, op0, op1))
+
+    def scaled(out, in_, c):
+        def fn(e, qn):
+            if qn == "v":
+                return e.tensor_scalar(ap(out), ap(in_), c, None, ALU.mult)
+            return e.activation(ap(out), ap(in_), ACT.Copy, 0.0, c)
+        add("vs", vc(out[2] - out[1]), [in_], [out], fn)
+
+    def tt(out, a, b, op, f=2.0, n=None):
+        add("v", vc(n or b[2] - b[1], f), [a, b], [out], lambda e: e.tensor_tensor(ap(out), ap(a), ap(b), op))
+
+    def memset(x, c):
+        add("v", vc(x[2] - x[1]), [], [x], lambda e: e.memset(ap(x), c))
+
+    def act(out, in_, func):
+        add("s", 0.065 + (in_[2] - in_[1]) * CYC, [in_], [out], lambda e: e.activation(ap(out), ap(in_), func))
+
+    gn = [0]
+
+    def gather(out, off):
+        q = GQ[gn[0] % len(GQ)]
+        gn[0] += 1
+
+        def fn(e, qn):
+            src = T.FL[:, 0:W].indirect(ap(off))
+            return e.tensor_copy(ap(out), src) if qn == "v" else e.activation(ap(out), src, ACT.Copy)
+        add(q, 0.06 + (out[2] - out[1]) * CYC * GAM, [("FL", 0, W), off], [out], lambda e: fn(e, "v" if q == "v" else "s"))
+        if len(q) == 2:
+            ops[-1]["fn"] = fn
+
+    def mm(out, terms):
+        def fn(e):
+            ins = None
+            for k, (l, r) in enumerate(terms):
+                ins = e.matmul(ap(out), ap(l), ap(r), k == 0, k == len(terms) - 1)
+            return ins
+        cost = 0.0
+        for l, r in terms:
+            n = (r[2] - r[1] + (r[3] if len(r) > 3 else 1) - 1) // (r[3] if len(r) > 3 else 1)
+            cost += max(64, n) * (4 if l[0] == "IF" else 1) * PEF * CYC
+        hull = {}
+        for x in [x for l, r in terms for x in (l, r)]:
+            c, d = hull.get(x[0], (x[1], x[2]))
+            hull[x[0]] = (min(c, x[1]), max(d, x[2]))
+        add("t", cost + 0.03, [(h, hull[h][0], hull[h][1]) for h in sorted(hull)], [out], fn)
+
+    def band(z, src, c0, n):
+        return [((z, 15 - p, 143 - p), (src, c0 + p, c0 + 16 * n, 16)) for p in range(16)]
+
+    def subtract(slot, a, b):
+        n = a[2] - a[1]
+        for c in range(0, n, 512):
+            d = min(n, c + 512)
+            mm((slot, c, d), [(("IP", 0, 128), (a[0], a[1] + c, a[1] + d)), (("IN", 0, 128), (b[0], b[1] + c, b[1] + d))])
+
+    def load(q, k, out, src):
+        add(q, 2.0 if k != 5 else 6.0, [], [out], lambda e: e.dma_start(ap(out), src), sem="ld%d" % k, inc=16)
+    load("y", 0, ("RI0", 0, P), T.riv[:, :])
+    load("sd", 1, ("MI0", 0, P), T.bord[:, :])
+    load("y", 5, ("FL", 0, W), T.flood[:, :])
+    load("sd", 2, ("thi", 0, 1), T.th[:, :])
+    load("sd", 3, ("epi", 0, 1), T.eps[:, :])
+
+    memset(("ONE", 0, 144), 1.0)
+    add("g", 0.5, [], [("WI", 0, 144)], lambda e: e.iota(T.WI[:, :], [[1, 144]], 1, 0))
+    add("g", 0.5, [("ONE", 0, 128)], [("IP", 0, 128)],
+        lambda e: e.affine_select(T.IP[:, :], T.ONE[:, 0:128], [[-1, 128]], ALU.is_equal, 0.0, 0, 1))
+    ts(("WI", 0, 144), ("WI", 0, 144), 15, ALU.bitwise_and)
+    ts(("Z", 0, 144), ("WI", 0, 144), 0.0, ALU.is_equal)
+    add("g", 0.5, [("Z", 0, 144)], [("Z", 0, 144)],
+        lambda e: e.affine_select(T.Z[:, :], T.Z[:, :], [[-1, 144]], ALU.is_ge, 0.0, 15, 1))
+    add("g", 0.5, [("Z", 0, 144)], [("Z", 0, 144)],
+        lambda e: e.affine_select(T.Z[:, :], T.Z[:, :], [[1, 144]], ALU.is_ge, 0.0, 0, -1))
+    add("g", 0.8, [], [("WJ", 0, 320)], lambda e: e.iota(T.WJ[:, :], [[0, 64], [1, 5]], 0, 0))
+    ts(("RST", 0, 320), ("WJ", 0, 320), 0.0, ALU.is_equal)
+    ts(("RSK", 0, 320), ("RST", 0, 320), 67108864.0, ALU.mult, -33554432.0, ALU.add)
+    scaled(("RST", 0, 320), ("RSK", 0, 320), -1.0)
+    scaled(("IF", 0, 128), ("IP", 0, 128), 1.0)
+    scaled(("IN", 0, 128), ("IP", 0, 128), -1.0)
+    scaled(("IK", 0, 128), ("IP", 0, 128), 8192.0)
+    for m in range(4):
+        scaled(("IM%d" % m, 0, 128), ("IP", 0, 128), 8192.0 * (m - 4))
+    scaled(("ZK", 0, 144), ("Z", 0, 144), 8192.0)
+    scaled(("ZH", 0, 144), ("Z", 0, 144), float(H))
+    memset(("CP", 0, 64), 2048.0)
+    memset(("CN", 0, 64), -4096.0)
+    for m in range(4):
+        memset(("CC", 64 * m, 64 * m + 64), -4096.0 * (m - 4) ** 2)
+    memset(("CC", 256, 320), -7.5 * H)
+    memset(("KL", 0, 128), 0.0)
+    memset(("KR", 0, 320), 0.0)
+
+    def row(name, part, n, c):
+        add("v", vc(n), [], [(name, 0, n)], lambda e: e.memset(T[name][part:part + 1, 0:n], c))
+
+    def irow(name, part, n, pat):
+        add("g", 0.6, [], [(name, 0, n)],
+            lambda e: e.iota(T[name][part:part + 1, 0:n], pat, 0, 0, allow_small_or_imprecise_dtypes=True))
+    row("KL", 0, 128, 1.0)
+    row("KL", 32, 128, 1.0)
+    row("KL", 96, 128, 1.0)
+    row("KR", 64, 320, 1.0)
+    row("KR", 96, 320, -16777216.0)
+    irow("KL", 64, 128, [[0, 8], [1, 16]])
+    irow("KR", 0, 320, [[1024, 5], [0, 64]])
+    irow("KR", 32, 320, [[0, 5], [16, 64]])
+    add("g", 0.5, [], [("WK", 0, 128)], lambda e: e.iota(T.WK[:, :], [[1, 128]], 128, -1))
+    ts(("WK", 0, 128), ("WK", 0, 128), 15, ALU.bitwise_and)
+    ts(("DM", 0, 128), ("WK", 0, 128), 0.0, ALU.is_equal)
+    add("g", 0.2, [], [("K8", 0, 8)], lambda e: e.iota(T.K8[:, :], [[1, 8]], 185, 0, allow_small_or_imprecise_dtypes=True))
+    for k in range(2):
+        memset(("RA%d" % k, 200, 208), 0.0)
+        memset(("MA%d" % k, 192, 208), 0.0)
+        memset(("XR%d" % k, 3072, 3088), 0.0)
+        memset(("PF%d" % k, 192, 200), 0.0)
+        memset(("PM%d" % k, 0, 8), 0.0)
+    copy(("THR0", 0, 1), ("thi", 0, 1))
+    copy(("EPF", 0, 1), ("epi", 0, 1))
+
+    def from_r(t, a, b):
+        x = t % 2
+        ts(("RA%d" % x, 8 + a, 8 + b), ("RI%d" % x, a, b), 2048.0, ALU.subtract)
+        if a == 0:
+            ts(("RA%d" % x, 7, 8), ("RI%d" % x, 0, 1), 2048.0, ALU.subtract)
+        ts(("RV", a, b), ("RI%d" % x, a, b), 32.0, ALU.add)
+        ts(("RV", 192 + a, 192 + b), ("RI%d" % x, a, b), 3232.0, ALU.mult, float(65536 + 2464 * t - 8388608), ALU.add)
+
+    def from_m(t, a, b):
+        x = t % 2
+        copy(("MU%d" % x, a, b), ("MI%d" % x, a, b))
+        ts(("MA%d" % x, a, b), ("MI%d" % x, a, b), 2048.0, ALU.subtract)
+        ts(("MH%d" % x, a, b), ("MI%d" % x, a, b), 7.5 * H, ALU.add)
+
+    cnt = [0, 0, 0]
+
+    def temp():
+        cnt[2] += 1
+        return "TI%d" % (cnt[2] % 4)
+
+    def step1(t, a, b):
+        x, y = t % 2, cnt[0] % 2
+        cnt[0] += 1
+        n = b - a
+        N = ("XR%d" % x, 16 * (a + 1), 16 * (b + 1))
+        QF, QI, CI, CU, TS = ("%s%d" % (s, y) for s in ("QF", "QI", "CI", "CU", "TS"))
+        ABS, NOW, FB, KS, DS = ("%s%d" % (s, y) for s in ("ABS", "NOW", "FB", "KS", "DS"))
+        KI, KO, KU, NI, NB = ("%s%d" % (s, y) for s in ("KI", "KO", "KU", "NI", "NB"))
+        ra, ma = "RA%d" % x, "MA%d" % x
+        for m, (nm, o) in enumerate(((ra, 7 + a), (ra, 9 + a), (ma, a), (ma, a + 1))):
+            tt((QF, m * n, m * n + n), (nm, o, o + n), ("RV", a, b), ALU.mult, f=1.0)
+        for m in range(4):
+            tt((QI, m * n, m * n + n), (QF, m * n, m * n + n), ("RV", 192 + a, 192 + b), ALU.add, f=1.0)
+        ts((CI, 0, 4 * n), (QI, 0, 4 * n), 5, ALU.arith_shift_right, 4095, ALU.bitwise_and)
+        copy((CU, 0, 4 * n), (CI, 0, 4 * n))
+        subtract("SA", ("XR%d" % x, 16 * a, 16 * b), N)
+        act((NOW, 0, 16 * n), ("SA", 0, 16 * n), ACT.Abs)
+        subtract("SA", ("XM%d" % x, 16 * a, 16 * b), N)
+        act((ABS, 4096, 4096 + 16 * n), ("SA", 0, 16 * n), ACT.Abs)
+        for m in range(4):
+            d0 = 1024 * (cnt[1] % 4)
+            cnt[1] += 1
+            off, out = (CU, m * n, m * n + n), ("XD", d0, d0 + 16 * n)
+            if m in PLAIN[(cnt[0] - 1) % len(PLAIN)]:
+                gather(out, off)
+                subtract("SA", out, N)
+                act((ABS, 1024 * m, 1024 * m + 16 * n), ("SA", 0, 16 * n), ACT.Abs)
+                continue
+            add("v", 0.06 + 16 * n * CYC * GAM, [("FL", 0, W), off, N], [out],
+                lambda e, o=out, f=off: e.tensor_tensor(ap(o), T.FL[:, 0:W].indirect(ap(f)), ap(N), ALU.subtract))
+            act((ABS, 1024 * m, 1024 * m + 16 * n), out, ACT.Abs)
+        for m in (4, 0, 1, 2, 3):
+            mm(("KY", m, 5 * n, 5), [(("KL", 0, 128), ("KR", 64 * m, 64 * m + n))] + band("ZK", ABS, 1024 * m, n))
+        add("v", vc(5 * n), [("RSK", 0, 5 * n), ("KY", 0, 5 * n)], [(KS, 0, 5 * n)],
+            lambda e: e.tensor_tensor_scan(T[KS][:, 0:5 * n], T.RSK[:, 0:5 * n], T.KY[:, 0:5 * n], 0.0, ALU.max, ALU.min))
+        copy((KI, 0, n), (KS, 4, 5 * n, 5), f=1.0)
+        ts((KO, 0, n), (KI, 0, n), 8191, ALU.bitwise_and)
+        copy((KU, 0, n), (KO, 0, n))
+        ts((NI, 0, n), (KI, 0, n), 10, ALU.arith_shift_right, 7, ALU.bitwise_and)
+        ts((NB, 0, n), (NI, 0, n), 4.0, ALU.subtract)
+        add("v", 0.06 + 16 * n * CYC * GAM, [(ABS, 0, 5120 - 1024 + 16 * n), (KU, 0, n), (NOW, 0, 16 * n)], [(FB, 0, 16 * n)],
+            lambda e: e.tensor_tensor(T[FB][:, 0:16 * n], T[ABS][:, 0:4096 + 16 * n].indirect(T[KU][:, 0:n]), T[NOW][:, 0:16 * n], ALU.is_ge))
+        for m in range(4):
+            mm(("TB", m * n, m * n + n), [(("IP", 0, 128), ("CC", 64 * m, 64 * m + n)), (("IM%d" % m, 0, 128), (NB, 0, n))])
+            tt((TS, m, 5 * n, 5), ("TB", m * n, m * n + n), (CI, m * n, m * n + n), ALU.add, f=1.0)
+        copy((TS, 4, 5 * n, 5), ("MI%d" % x, a, b))
+        add("v", vc(5 * n), [("RST", 0, 5 * n), (TS, 0, 5 * n)], [(DS, 0, 5 * n)],
+            lambda e: e.tensor_tensor_scan(T[DS][:, 0:5 * n], T.RST[:, 0:5 * n], T[TS][:, 0:5 * n], 0.0, ALU.min, ALU.max))
+        mm(("TB", 320, 320 + n), [(("IF", 0, 128), (ra, 8 + a, 8 + b)), (("IP", 0, 128), ("CP", 0, n)), (("IP", 0, 128), ("CC", 256, 256 + n))]
+           + band("ZH", FB, 0, n))
+        pi, ti = "PI%d" % x, temp()
+        tt((ti, 0, n), ("TB", 320, 320 + n), (DS, 4, 5 * n, 5), ALU.max, f=1.0, n=n)
+        ts((pi, a, b), (ti, 0, n), 4095, ALU.bitwise_and)
+        if b == P:
+            copy((pi, P - 1, P), ("RI%d" % x, P - 1, P))
+        copy(("PU%d" % x, a, b), (pi, a, b))
+        copy(("PF%d" % x, a, b), (pi, a, b))
+        gather(("XP", 16 * a, 16 * b), ("PU%d" % x, a, b))
+
+    def neck(t, a, b):
+        x, y, n = t % 2, cnt[0] % 2, b - a
+        NA, OK, PM, pf = "NA%d" % y, "OK%d" % y, "PM%d" % x, "PF%d" % x
+        subtract("SB", ("XP", 16 * a, 16 * b), ("XP", 16 * a + 128, 16 * b + 128))
+        act((NA, 0, 16 * n), ("SB", 0, 16 * n), ACT.Abs)
+        mm(("MS", 0, n), band("Z", NA, 0, n))
+        ts((OK, 0, n), ("MS", 0, n), ("THR%d" % t, 0, 1), ALU.is_lt)
+        add("v", vc(n), [(OK, 0, n), (PM, 7 + a, 8 + a)], [(PM, 8 + a, 8 + b)],
+            lambda e: e.tensor_tensor_scan(T[PM][:, 8 + a:8 + b], T[OK][:, 0:n], T[OK][:, 0:n], T[PM][:, 7 + a:8 + a], ALU.max, ALU.max))
+        mm(("MS", 64, 64 + n), [(("IF", 0, 128), (pf, a + 8, b + 8)), (("IP", 0, 128), ("CN", 0, n)), (("IK", 0, 128), (PM, 7 + a, 7 + b))])
+        ti = temp()
+        tt((ti, 0, n), ("MS", 64, 64 + n), (pf, a, b), ALU.max, f=1.0)
+        new_r(t, a, b, ti)
+
+    def new_r(t, a, b, src):
+        x1, n = (t + 1) % 2, b - a
+        ts(("RI%d" % x1, a, b), (src, 0, n), 4095, ALU.bitwise_and)
+        copy(("RU%d" % x1, a, b), ("RI%d" % x1, a, b))
+        gather(("XR%d" % x1, 16 * a, 16 * b), ("RU%d" % x1, a, b))
+        if t < RO - 1:
+            from_r(t + 1, a, b)
+        else:
+            copy(("OUTR", a, b), ("RI%d" % x1, a, b))
+            ts(("RA%d" % x1, 8 + a, 8 + b), ("RI%d" % x1, a, b), 2048.0, ALU.subtract)
+        border(t, a, b)
+
+    def border(t, a, b):
+        x, x1, y, n = t % 2, (t + 1) % 2, cnt[0] % 2, b - a
+        MX, MB = "MX%d" % y, "MB%d" % y
+        subtract("SB", ("XR%d" % x1, 16 * a, 16 * b), ("XM%d" % x, 16 * a, 16 * b))
+        act((MX, 0, 16 * n), ("SB", 0, 16 * n), ACT.Abs)
+        ts((MB, 0, 16 * n), (MX, 0, 16 * n), ("EPF", 0, 1), ALU.is_gt, f=0.5)
+        mm(("KY", 320, 320 + n), [(("IF", 0, 128), ("RA%d" % x1, 8 + a, 8 + b)), (("IP", 0, 128), ("CP", 0, n))] + band("ZH", MB, 0, n))
+        ti = temp()
+        tt((ti, 0, n), ("KY", 320, 320 + n), ("MH%d" % x, a, b), ALU.min, f=1.0)
+        ts(("MI%d" % x1, a, b), (ti, 0, n), 4095, ALU.bitwise_and)
+        if t < RO - 1:
+            from_m(t + 1, a, b)
+            gather(("XM%d" % x1, 16 * a, 16 * b), ("MU%d" % x1, a, b))
+        else:
+            copy(("OUTM", a, b), ("MI%d" % x1, a, b))
+
+    def loops(t):
+        x, PM, pf = t % 2, "PM%d" % (t % 2), "PF%d" % (t % 2)
+        add("v", vc(184), [(PM, 8, 192)], [("SPM", 0, 1)],
+            lambda e: e.tensor_reduce(T.SPM[:, :], T[PM][:, 8:192], AxisListType.X, ALU.add))
+        ts(("OFF", 0, 8), ("K8", 0, 8), ("SPM", 0, 1), ALU.subtract)
+        add("v", 0.3, [("OFF", 0, 8), (pf, 0, 200)], [("LG", 0, 128)],
+            lambda e: e.tensor_copy(T.LG[:, :], T[pf][:, 0:200].indirect(T.OFF[:, 0:8])))
+        tt(("LM", 0, 128), ("LG", 0, 128), ("DM", 0, 128), ALU.mult)
+        src = "LM"
+        for w, dst in ((64, "L64"), (32, "L32"), (16, "L16"), (8, "LO")):
+            tt((dst, 0, w), (src, 0, 2 * w, 2), (src, 1, 2 * w, 2), ALU.add, n=w)
+            src = dst
+        ts(("SND%d" % t, 0, 8), ("LO", 0, 8), 4096.0, ALU.add, (PM, 191, 192), ALU.mult)
+        dst = T.cores[(rank + 1 + t % 3) % len(T.cores)]
+        eng = topo.engines(core, dst)[:8]
+        msk = 0
+        for q in eng:
+            msk |= 1 << q
+        rid, pid = topo.addr(dst, core)
+        send = add("g", 0.5, [("SND%d" % t, 0, 8)], [],
+                   lambda e: e.remote_dma(T["LAND%d" % t][:, :], T["SND%d" % t][:, :], T.sem["arr%d" % t], T.sem.sent, pid, rid, msk),
+                   sem="sent", inc=len(eng), free=True)
+        src_core = T.cores[(rank - 1 - t % 3) % len(T.cores)]
+        add("x", 4.0, [], [("LAND%d" % t, 0, 8)], None, sem="arr%d" % t, inc=len(topo.engines(src_core, core)[:8]), after=[send])
+        ts(("NPM", 0, 1), (PM, 191, 192), -1.0, ALU.mult, 1.0, ALU.add)
+        ts(("RTK", 0, 8), (pf, 184, 192), 8192.0, ALU.add, ("NPM", 0, 1), ALU.mult)
+        tt(("BASE", 0, 8), ("LO", 0, 8), ("RTK", 0, 8), ALU.max)
+        ts(("THR%d" % (t + 1), 0, 1), (PM, 191, 192), 16.0, ALU.mult, ("THR%d" % t, 0, 1), ALU.add)
+
+    def tail(t):
+        ti = temp()
+        tt((ti, 0, 8), ("BASE", 0, 8), ("LAND%d" % t, 0, 8), ALU.max)
+        new_r(t, 184, 192, ti)
+
+    def store(k, out, src):
+        add("y", 2.0, [src], [], lambda e: e.dma_start(out, ap(src)), sem="st%d" % k, inc=16, free=True)
+
+    copy(("RU0", 0, P), ("RI0", 0, P))
+    from_r(0, 0, P)
+    from_m(0, 0, P)
+    bs = CH[0]
+    for a, b in zip([0] + bs[:-1], bs):
+        gather(("XR0", 16 * a, 16 * b), ("RU0", a, b))
+        gather(("XM0", 16 * a, 16 * b), ("MU0", a, b))
+    chunks = [(t, a, b) for t in range(RO) for a, b in zip([0] + CH[t][:-1], CH[t])]
+
+    def rest(c):
+        t, a, b = c
+        neck(t, max(a - 8, 0), b - 8)
+        if b == P:
+            loops(t)
+            if t == RO - 1:
+                store(0, T.yr[:, 0:184], ("OUTR", 0, 184))
+                store(1, T.ym[:, 0:184], ("OUTM", 0, 184))
+                ts(("OUTA", 0, 1), ("THR3", 0, 1), ("THR0", 0, 1), ALU.subtract, 0.0625, ALU.mult)
+                store(2, T.ya[:, :], ("OUTA", 0, 1))
+            tail(t)
+    for k, c in enumerate(chunks):
+        step1(*c)
+        if k:
+            rest(chunks[k - 1])
+    rest(chunks[-1])
+    store(3, T.yr[:, 184:192], ("OUTR", 184, 192))
+    store(4, T.ym[:, 184:192], ("OUTM", 184, 192))
+    return ops
+
+
+def depend(ops):
+    hist = {}
+    deps = []
+    for k, o in enumerate(ops):
+        d = {}
+        for lst, w in ((o["r"], False), (o["w"], True)):
+            for x in lst:
+                n, a, b = x[0], x[1], x[2]
+                for (j, c, e, ww) in hist.get(n, ()):
+                    if j == k:
+                        continue
+                    hit = a < e and c < b
+                    if hit and (w or ww):
+                        raw = ww
+                        if raw or j not in d:
+                            d[j] = d.get(j, False) or raw
+        for lst, w in ((o["r"], False), (o["w"], True)):
+            for x in lst:
+                n, a, b = x[0], x[1], x[2]
+                h = hist.setdefault(n, [])
+                if w and len(x) == 3 and SCRATCH[n][0] != "psum":
+                    h[:] = [z for z in h if z[0] == k or not (a <= z[1] and z[2] <= b)]
+                h.append((k, a, b, w))
+        deps.append(d)
+    return deps
+
+
+def schedule(ops, deps):
+    n = len(ops)
+    users = [[] for _ in range(n)]
+    for k, d in enumerate(deps):
+        for j in d:
+            users[j].append(k)
+        for j in ops[k]["after"]:
+            users[j].append(k)
+    rank = [0.0] * n
+    for k in range(n - 1, -1, -1):
+        rank[k] = ops[k]["cost"] + max([rank[u] + WAKE for u in users[k]], default=0.0)
+    left = [len(set(list(deps[k]) + ops[k]["after"])) for k in range(n)]
+    done, start, qof = [None] * n, [None] * n, [None] * n
+    ready = [k for k in range(n) if left[k] == 0]
+    rt = [0.0] * n
+    free = {q: 0.0 for q in ("v", "s", "t", "g", "y", "x")}
+    order = []
+    lats = {}
+    banks = [sorted({(x[0], c) for x in o["r"] + o["w"] if SCRATCH[x[0]][0] == "psum"
+                     for c in range(x[1] // 512, (x[2] - 1) // 512 + 1)}) for o in ops]
+    user = {}
+
+    def held(k, q):
+        return [j for b in banks[k] for p, j in user.get(b, {}).items() if p != q]
+
+    def latest(k, q):
+        lat = 0.0
+        for j in deps[k]:
+            if qof[j] != q:
+                lat = max(lat, done[j] + WAKE)
+            elif deps[k][j]:
+                lat = max(lat, done[j] + WAKE * 0.6)
+        for j in ops[k]["after"]:
+            lat = max(lat, done[j])
+        return lat
+    rng = np.random.RandomState(SEED)
+    rank = [r - AGE * k for k, r in enumerate(rank)]
+    if NOISE:
+        rank = [r + 100 * NOISE * float(z) for r, z in zip(rank, rng.randn(n))]
+    while ready:
+        best = None
+        for q in free:
+            cand = []
+            for k in ready:
+                if q in ("s" if ops[k]["q"] == "sd" else ops[k]["q"]):
+                    if (k, q) not in lats:
+                        lats[k, q] = latest(k, q)
+                    s = max(free[q], lats[k, q])
+                    if banks[k]:
+                        s = max([s] + [done[j] + WAKE for j in held(k, q)])
+                    cand.append((s, k))
+            if cand:
+                lim = min(cand)[0] + SLACK
+                s, k = max(((rank[k], s, k) for s, k in cand if s <= lim))[1:]
+                if best is None or s < best[0]:
+                    best = (s, k, q)
+        s, k, q = best
+        ready.remove(k)
+        for j in held(k, q):
+            deps[k].setdefault(j, False)
+        for b in banks[k]:
+            user.setdefault(b, {})[q] = k
+        start[k], qof[k] = s, q
+        issue = 0.06 if ops[k]["q"] in ("y", "sd") else ops[k]["cost"]
+        free[q] = s + issue if q != "x" else 0.0
+        done[k] = s + ops[k]["cost"]
+        order.append(k)
+        for u in set(users[k]):
+            left[u] -= 1
+            if left[u] == 0:
+                ready.append(u)
+    return order, qof, start, done
+
+
+def rank_program(g, core, T, topo):
+    if T.rank_of(core) is None:
+        return
+    ops = plan(core, T, topo)
+    deps = depend(ops)
+    order, qof, start, done = schedule(ops, deps)
+    eng = {"v": g.vector, "s": g.scalar, "t": g.tensor, "g": g, "y": g.sync}
+    total, mark, clock, pool = {}, {}, {}, []
+    known = {q: {} for q in eng}
+    for k in order:
+        o, q = ops[k], qof[k]
+        sem = o["sem"] or QSEM[q]
+        need = {}
+        if q == "x":
+            total[sem] = total.get(sem, 0) + o["inc"]
+            mark[k] = (sem, total[sem])
+            clock[k] = {sem: total[sem]}
+            continue
+        for j in deps[k]:
+            if qof[j] == q and (q == "t" or not deps[k][j]) and ops[j]["sem"] is None:
+                continue
+            s, v = mark[j]
+            if known[q].get(s, 0) < v:
+                if need.get(s, (0, 0))[0] < v:
+                    need[s] = (v, j)
+        if q == "g" and o["sem"] is None and pool:
+            s, v = mark[pool[-1]]
+            if known[q].get(s, 0) < v:
+                need[s] = (v, pool[-1])
+        if q == "g" and o["sem"] is None:
+            pool.append(k)
+        for s in sorted(need):
+            v, j = need[s]
+            if any(s2 != s and clock[need[s2][1]].get(s, 0) >= v for s2 in need):
+                continue
+            eng[q].wait_ge(T.sem[s], v)
+        for s in need:
+            v, j = need[s]
+            for s2, v2 in clock[j].items():
+                known[q][s2] = max(known[q].get(s2, 0), v2)
+        ins = o["fn"](eng[q], q) if o["q"] == "vs" else o["fn"](eng[q])
+        total[sem] = total.get(sem, 0) + o["inc"]
+        mark[k] = (sem, total[sem])
+        clock[k] = dict(known[q])
+        clock[k][sem] = total[sem]
+        if sem != "sent":
+            ins.then_inc(T.sem[sem], o["inc"])
+    for s in sorted(total):
+        if known["y"].get(s, 0) < total[s]:
+            g.sync.wait_ge(T.sem[s], total[s])

@@ -3,20 +3,22 @@ from concourse.mybir import AluOpType as ALU, AxisListType, ActivationFunctionTy
 
 W, P, L, RO = 4096, 192, 8, 3
 H = 262144
-CH = [[40, 80, 136, 192], [48, 96, 136, 192], [64, 88, 128, 192]]
+NM = 96
+SM = 16 * NM
+CH = [[76, 140, 192], [64, 128, 192], [48, 116, 192]]
 BF, F32, I32, U16 = "bfloat16", "float32", "int32", "uint16"
 
 SCRATCH = {
     "FL": ("sbuf", [128, W], BF),
     "ONE": ("sbuf", [128, 144], BF), "Z": ("sbuf", [128, 144], BF), "ZK": ("sbuf", [128, 144], BF), "ZH": ("sbuf", [128, 144], BF),
-    "WI": ("sbuf", [128, 144], I32), "WJ": ("sbuf", [128, 320], I32), "WK": ("sbuf", [128, 128], I32),
+    "WI": ("sbuf", [128, 144], I32), "WJ": ("sbuf", [128, 5 * NM], I32), "WK": ("sbuf", [128, 128], I32),
     "IP": ("sbuf", [128, 128], BF), "IN": ("sbuf", [128, 128], BF), "IK": ("sbuf", [128, 128], BF), "IF": ("sbuf", [128, 128], F32),
-    "KL": ("sbuf", [128, 128], BF), "KR": ("sbuf", [128, 320], BF), "CP": ("sbuf", [128, 64], BF), "CN": ("sbuf", [128, 64], BF), "CC": ("sbuf", [128, 320], BF),
-    "RSK": ("sbuf", [128, 320], F32), "RST": ("sbuf", [128, 320], F32), "DM": ("sbuf", [128, 128], F32), "K8": ("sbuf", [128, 8], F32),
+    "KL": ("sbuf", [128, 128], BF), "KR": ("sbuf", [128, 5 * NM], BF), "CP": ("sbuf", [128, NM], BF), "CN": ("sbuf", [128, NM], BF),
+    "CC": ("sbuf", [128, 5 * NM], BF), "RSK": ("sbuf", [128, 5 * NM], F32), "RST": ("sbuf", [128, 5 * NM], F32), "DM": ("sbuf", [128, 128], F32), "K8": ("sbuf", [128, 8], F32),
     "thi": ("sbuf", [128, 1], I32), "epi": ("sbuf", [128, 1], I32), "EPF": ("sbuf", [128, 1], F32),
     "OUTR": ("sbuf", [128, P], F32), "OUTM": ("sbuf", [128, P], F32), "OUTA": ("sbuf", [128, 1], F32),
-    "LG": ("sbuf", [128, 128], F32), "LM": ("sbuf", [128, 128], F32), "L64": ("sbuf", [128, 64], F32), "L32": ("sbuf", [128, 32], F32),
-    "L16": ("sbuf", [128, 16], F32), "LO": ("sbuf", [128, 8], F32), "SPM": ("sbuf", [128, 1], F32), "OFF": ("sbuf", [128, 8], U16),
+    "LG": ("sbuf", [128, 128], F32), "LM": ("sbuf", [128, 128], F32), "RSL": ("sbuf", [128, 128], F32),
+    "SPM": ("sbuf", [128, 1], F32), "OFF": ("sbuf", [128, 8], U16),
     "NPM": ("sbuf", [128, 1], F32), "RTK": ("sbuf", [128, 8], F32), "BASE": ("sbuf", [128, 8], F32),
     "SA": ("psum", [128, 1024], F32), "SB": ("psum", [128, 1024], F32), "KY": ("psum", [128, 512], F32),
     "TB": ("psum", [128, 512], F32), "MS": ("psum", [128, 512], F32), "RV": ("psum", [128, 512], F32),
@@ -29,37 +31,41 @@ for _t in range(RO):
 for _t in range(RO + 1):
     SCRATCH["THR%d" % _t] = ("sbuf", [128, 1], F32)
 for _k in range(2):
-    for _n, _w, _d in (("XR", 3088, BF), ("XM", 3072, BF), ("ABS", 5120, BF), ("NOW", 1024, BF), ("FB", 1024, BF), ("NA", 1024, BF),
-                       ("MX", 1024, BF), ("MB", 1024, BF), ("QF", 256, F32), ("QI", 256, I32), ("CI", 256, I32), ("CU", 256, U16),
-                       ("TS", 320, F32), ("KS", 320, F32), ("KI", 64, I32), ("KO", 64, I32), ("KU", 64, U16), ("NI", 64, I32),
-                       ("NB", 64, BF), ("DS", 320, F32), ("OK", 64, BF), ("RI", P, I32), ("RU", P, U16), ("RA", 208, F32),
+    for _n, _w, _d in (("XR", 3088, BF), ("XM", 3072, BF), ("ABS", 5 * SM, BF), ("NOW", SM, BF), ("FB", SM, BF), ("NA", SM, BF),
+                       ("MX", SM, BF), ("MB", SM, BF), ("QF", 4 * NM, F32), ("QI", 4 * NM, I32), ("CI", 4 * NM, I32), ("CU", 4 * NM, U16),
+                       ("TS", 5 * NM, F32), ("KS", 5 * NM, F32), ("KI", NM, I32), ("KO", NM, I32), ("KU", NM, U16), ("NI", NM, I32),
+                       ("NB", NM, BF), ("DS", 5 * NM, F32), ("OK", NM, BF), ("RI", P, I32), ("RU", P, U16), ("RA", 208, F32),
                        ("MI", P, I32), ("MU", P, U16), ("MA", 208, F32), ("MH", P, F32), ("PI", P, I32), ("PU", P, U16),
                        ("PF", 200, F32), ("PM", 208, BF)):
         SCRATCH["%s%d" % (_n, _k)] = ("sbuf", [128, _w], _d)
 SCRATCH["XP"] = ("sbuf", [128, 3072], BF)
-SCRATCH["XD"] = ("sbuf", [128, 4096], BF)
+SCRATCH["XD"] = ("sbuf", [128, 4 * SM], BF)
 
 for _k in range(4):
-    SCRATCH["TI%d" % _k] = ("sbuf", [128, 64], I32)
+    SCRATCH["TI%d" % _k] = ("sbuf", [128, NM], I32)
 QSEM = {"v": "cv", "s": "cs", "t": "ct", "g": "cg"}
-SEMAPHORES = ["cv", "cs", "ct", "cg", "sent", "arr0", "arr1", "arr2"] + ["ld%d" % k for k in range(6)] + ["st%d" % k for k in range(8)]
+SEMAPHORES = ["cv", "cs", "ct", "cg", "sent", "arr0", "arr1", "arr2"] + ["ld%d" % k for k in range(6)] + ["st%d" % k for k in range(8)] + ["ac%d" % k for k in range(32)]
 CYC = 0.83e-3 * 1.25
 GAM = 1.5
 WAKE = 0.08
-SLACK, NOISE, SEED = 0.0, 0.0, 0
-PLAIN = [()]
+SLACK, NOISE, SEED = 0.0, 0.003, 991
+PLAIN = [(), (0,), (1,), (0,), (3,), (), (1,), (), (3,), (1,)]
 PEF = 0.5
 AGE = 0.0
-GQ = [{"x": "vs"}.get(c, c) for c in "xsvxssssssssssssxssssxsxssssssssssxvsssssvxsvsssss"]
+UNIT = 512
+FUSE = 40
+GQ = [{"x": "vs"}.get(c, c) for c in "ssxvsssxsssvssxsssvssxssxsxxxxsxssxsvssvvsvvssvv"]
 
 
 def plan(core, T, topo):
     ops = []
     rank = T.rank_of(core)
 
-    def add(q, cost, reads, writes, fn, sem=None, inc=1, after=(), free=False):
+    def add(q, cost, reads, writes, fn, sem=None, inc=1, after=(), iss=None):
+        if iss is None:
+            iss = 0.06 if q in ("y", "sd") else cost
         ops.append({"q": q, "cost": cost, "r": reads, "w": writes, "fn": fn, "sem": sem, "inc": inc, "after": list(after),
-                    "free": free})
+                    "iss": iss})
         return len(ops) - 1
 
     def ap(x):
@@ -135,6 +141,22 @@ def plan(core, T, topo):
             d = min(n, c + 512)
             mm((slot, c, d), [(("IP", 0, 128), (a[0], a[1] + c, a[1] + d)), (("IN", 0, 128), (b[0], b[1] + c, b[1] + d))])
 
+    turn = [0]
+
+    def size(slot, a, b, out):
+        n = a[2] - a[1]
+        if n <= UNIT:
+            subtract(slot, a, b)
+            act(out, (slot, 0, n), ACT.Abs)
+            return
+        h = (n // -(-n // 512) + 15) // 16 * 16
+        for c in range(0, n, h):
+            d = min(n, c + h)
+            o = 512 * (turn[0] % 2)
+            turn[0] += 1
+            mm((slot, o, o + d - c), [(("IP", 0, 128), (a[0], a[1] + c, a[1] + d)), (("IN", 0, 128), (b[0], b[1] + c, b[1] + d))])
+            act((out[0], out[1] + c, out[1] + d), (slot, o, o + d - c), ACT.Abs)
+
     def load(q, k, out, src):
         add(q, 2.0 if k != 5 else 6.0, [], [out], lambda e: e.dma_start(ap(out), src), sem="ld%d" % k, inc=16)
     load("y", 0, ("RI0", 0, P), T.riv[:, :])
@@ -153,10 +175,10 @@ def plan(core, T, topo):
         lambda e: e.affine_select(T.Z[:, :], T.Z[:, :], [[-1, 144]], ALU.is_ge, 0.0, 15, 1))
     add("g", 0.5, [("Z", 0, 144)], [("Z", 0, 144)],
         lambda e: e.affine_select(T.Z[:, :], T.Z[:, :], [[1, 144]], ALU.is_ge, 0.0, 0, -1))
-    add("g", 0.8, [], [("WJ", 0, 320)], lambda e: e.iota(T.WJ[:, :], [[0, 64], [1, 5]], 0, 0))
-    ts(("RST", 0, 320), ("WJ", 0, 320), 0.0, ALU.is_equal)
-    ts(("RSK", 0, 320), ("RST", 0, 320), 67108864.0, ALU.mult, -33554432.0, ALU.add)
-    scaled(("RST", 0, 320), ("RSK", 0, 320), -1.0)
+    add("g", 1.0, [], [("WJ", 0, 5 * NM)], lambda e: e.iota(T.WJ[:, :], [[0, NM], [1, 5]], 0, 0))
+    ts(("RST", 0, 5 * NM), ("WJ", 0, 5 * NM), 0.0, ALU.is_equal)
+    ts(("RSK", 0, 5 * NM), ("RST", 0, 5 * NM), 67108864.0, ALU.mult, -33554432.0, ALU.add)
+    scaled(("RST", 0, 5 * NM), ("RSK", 0, 5 * NM), -1.0)
     scaled(("IF", 0, 128), ("IP", 0, 128), 1.0)
     scaled(("IN", 0, 128), ("IP", 0, 128), -1.0)
     scaled(("IK", 0, 128), ("IP", 0, 128), 8192.0)
@@ -164,13 +186,13 @@ def plan(core, T, topo):
         scaled(("IM%d" % m, 0, 128), ("IP", 0, 128), 8192.0 * (m - 4))
     scaled(("ZK", 0, 144), ("Z", 0, 144), 8192.0)
     scaled(("ZH", 0, 144), ("Z", 0, 144), float(H))
-    memset(("CP", 0, 64), 2048.0)
-    memset(("CN", 0, 64), -4096.0)
+    memset(("CP", 0, NM), 2048.0)
+    memset(("CN", 0, NM), -4096.0)
     for m in range(4):
-        memset(("CC", 64 * m, 64 * m + 64), -4096.0 * (m - 4) ** 2)
-    memset(("CC", 256, 320), -7.5 * H)
+        memset(("CC", NM * m, NM * m + NM), -4096.0 * (m - 4) ** 2)
+    memset(("CC", 4 * NM, 5 * NM), -7.5 * H)
     memset(("KL", 0, 128), 0.0)
-    memset(("KR", 0, 320), 0.0)
+    memset(("KR", 0, 5 * NM), 0.0)
 
     def row(name, part, n, c):
         add("v", vc(n), [], [(name, 0, n)], lambda e: e.memset(T[name][part:part + 1, 0:n], c))
@@ -181,14 +203,15 @@ def plan(core, T, topo):
     row("KL", 0, 128, 1.0)
     row("KL", 32, 128, 1.0)
     row("KL", 96, 128, 1.0)
-    row("KR", 64, 320, 1.0)
-    row("KR", 96, 320, -16777216.0)
+    row("KR", 64, 5 * NM, 1.0)
+    row("KR", 96, 5 * NM, -16777216.0)
     irow("KL", 64, 128, [[0, 8], [1, 16]])
-    irow("KR", 0, 320, [[1024, 5], [0, 64]])
-    irow("KR", 32, 320, [[0, 5], [16, 64]])
+    irow("KR", 0, 5 * NM, [[SM, 5], [0, NM]])
+    irow("KR", 32, 5 * NM, [[0, 5], [16, NM]])
     add("g", 0.5, [], [("WK", 0, 128)], lambda e: e.iota(T.WK[:, :], [[1, 128]], 128, -1))
     ts(("WK", 0, 128), ("WK", 0, 128), 15, ALU.bitwise_and)
     ts(("DM", 0, 128), ("WK", 0, 128), 0.0, ALU.is_equal)
+    ts(("RSL", 0, 128), ("WI", 15, 143), 0.0, ALU.not_equal)
     add("g", 0.2, [], [("K8", 0, 8)], lambda e: e.iota(T.K8[:, :], [[1, 8]], 185, 0, allow_small_or_imprecise_dtypes=True))
     for k in range(2):
         memset(("RA%d" % k, 200, 208), 0.0)
@@ -213,7 +236,7 @@ def plan(core, T, topo):
         ts(("MA%d" % x, a, b), ("MI%d" % x, a, b), 2048.0, ALU.subtract)
         ts(("MH%d" % x, a, b), ("MI%d" % x, a, b), 7.5 * H, ALU.add)
 
-    cnt = [0, 0, 0]
+    cnt = [0, 0, 0, 0]
 
     def temp():
         cnt[2] += 1
@@ -232,45 +255,48 @@ def plan(core, T, topo):
             tt((QF, m * n, m * n + n), (nm, o, o + n), ("RV", a, b), ALU.mult, f=1.0)
         for m in range(4):
             tt((QI, m * n, m * n + n), (QF, m * n, m * n + n), ("RV", 192 + a, 192 + b), ALU.add, f=1.0)
-        ts((CI, 0, 4 * n), (QI, 0, 4 * n), 5, ALU.arith_shift_right, 4095, ALU.bitwise_and)
-        copy((CU, 0, 4 * n), (CI, 0, 4 * n))
-        subtract("SA", ("XR%d" % x, 16 * a, 16 * b), N)
-        act((NOW, 0, 16 * n), ("SA", 0, 16 * n), ACT.Abs)
-        subtract("SA", ("XM%d" % x, 16 * a, 16 * b), N)
-        act((ABS, 4096, 4096 + 16 * n), ("SA", 0, 16 * n), ACT.Abs)
+        for h in (0, 2 * n):
+            ts((CI, h, h + 2 * n), (QI, h, h + 2 * n), 5, ALU.arith_shift_right, 4095, ALU.bitwise_and)
+            copy((CU, h, h + 2 * n), (CI, h, h + 2 * n))
+        size("SA", ("XR%d" % x, 16 * a, 16 * b), N, (NOW, 0, 16 * n))
+        size("SA", ("XM%d" % x, 16 * a, 16 * b), N, (ABS, 4 * SM, 4 * SM + 16 * n))
         for m in range(4):
-            d0 = 1024 * (cnt[1] % 4)
+            d0 = SM * (cnt[1] % 4)
             cnt[1] += 1
             off, out = (CU, m * n, m * n + n), ("XD", d0, d0 + 16 * n)
             if m in PLAIN[(cnt[0] - 1) % len(PLAIN)]:
-                gather(out, off)
-                subtract("SA", out, N)
-                act((ABS, 1024 * m, 1024 * m + 16 * n), ("SA", 0, 16 * n), ACT.Abs)
+                add("s", 0.065 + 16 * n * CYC * GAM, [("FL", 0, W), off], [out],
+                    lambda e, o=out, f=off: e.activation(ap(o), T.FL[:, 0:W].indirect(ap(f)), ACT.Copy, 0.0, -1.0))
+                add("g", 3.5, [out, N], [out], lambda e, o=out: e.dma_start(ap(o), ap(N), accum_op=ALU.add),
+                    sem="ac%d" % cnt[3], inc=16, iss=1.1)
+                cnt[3] += 1
+                act((ABS, SM * m, SM * m + 16 * n), out, ACT.Abs)
                 continue
             add("v", 0.06 + 16 * n * CYC * GAM, [("FL", 0, W), off, N], [out],
                 lambda e, o=out, f=off: e.tensor_tensor(ap(o), T.FL[:, 0:W].indirect(ap(f)), ap(N), ALU.subtract))
-            act((ABS, 1024 * m, 1024 * m + 16 * n), out, ACT.Abs)
+            act((ABS, SM * m, SM * m + 16 * n), out, ACT.Abs)
         for m in (4, 0, 1, 2, 3):
-            mm(("KY", m, 5 * n, 5), [(("KL", 0, 128), ("KR", 64 * m, 64 * m + n))] + band("ZK", ABS, 1024 * m, n))
+            mm(("KY", m, 5 * n, 5), [(("KL", 0, 128), ("KR", NM * m, NM * m + n))] + band("ZK", ABS, SM * m, n))
         add("v", vc(5 * n), [("RSK", 0, 5 * n), ("KY", 0, 5 * n)], [(KS, 0, 5 * n)],
             lambda e: e.tensor_tensor_scan(T[KS][:, 0:5 * n], T.RSK[:, 0:5 * n], T.KY[:, 0:5 * n], 0.0, ALU.max, ALU.min))
         copy((KI, 0, n), (KS, 4, 5 * n, 5), f=1.0)
         ts((KO, 0, n), (KI, 0, n), 8191, ALU.bitwise_and)
         copy((KU, 0, n), (KO, 0, n))
-        ts((NI, 0, n), (KI, 0, n), 10, ALU.arith_shift_right, 7, ALU.bitwise_and)
+        ts((NI, 0, n), (KO, 0, n), 1.0 / SM, ALU.mult, -0.4995, ALU.add)
         ts((NB, 0, n), (NI, 0, n), 4.0, ALU.subtract)
-        add("v", 0.06 + 16 * n * CYC * GAM, [(ABS, 0, 5120 - 1024 + 16 * n), (KU, 0, n), (NOW, 0, 16 * n)], [(FB, 0, 16 * n)],
-            lambda e: e.tensor_tensor(T[FB][:, 0:16 * n], T[ABS][:, 0:4096 + 16 * n].indirect(T[KU][:, 0:n]), T[NOW][:, 0:16 * n], ALU.is_ge))
+        add("v", 0.06 + 16 * n * CYC * GAM, [(ABS, 0, 4 * SM + 16 * n), (KU, 0, n), (NOW, 0, 16 * n)], [(FB, 0, 16 * n)],
+            lambda e: e.tensor_tensor(T[FB][:, 0:16 * n], T[ABS][:, 0:4 * SM + 16 * n].indirect(T[KU][:, 0:n]), T[NOW][:, 0:16 * n], ALU.is_ge))
         for m in range(4):
-            mm(("TB", m * n, m * n + n), [(("IP", 0, 128), ("CC", 64 * m, 64 * m + n)), (("IM%d" % m, 0, 128), (NB, 0, n))])
+            mm(("TB", m * n, m * n + n), [(("IP", 0, 128), ("CC", NM * m, NM * m + n)), (("IM%d" % m, 0, 128), (NB, 0, n))])
             tt((TS, m, 5 * n, 5), ("TB", m * n, m * n + n), (CI, m * n, m * n + n), ALU.add, f=1.0)
         copy((TS, 4, 5 * n, 5), ("MI%d" % x, a, b))
         add("v", vc(5 * n), [("RST", 0, 5 * n), (TS, 0, 5 * n)], [(DS, 0, 5 * n)],
             lambda e: e.tensor_tensor_scan(T[DS][:, 0:5 * n], T.RST[:, 0:5 * n], T[TS][:, 0:5 * n], 0.0, ALU.min, ALU.max))
-        mm(("TB", 320, 320 + n), [(("IF", 0, 128), (ra, 8 + a, 8 + b)), (("IP", 0, 128), ("CP", 0, n)), (("IP", 0, 128), ("CC", 256, 256 + n))]
+        mm(("TB", 400, 400 + n), [(("IF", 0, 128), (ra, 8 + a, 8 + b)), (("IP", 0, 128), ("CP", 0, n)),
+                                  (("IP", 0, 128), ("CC", 4 * NM, 4 * NM + n))]
            + band("ZH", FB, 0, n))
         pi, ti = "PI%d" % x, temp()
-        tt((ti, 0, n), ("TB", 320, 320 + n), (DS, 4, 5 * n, 5), ALU.max, f=1.0, n=n)
+        tt((ti, 0, n), ("TB", 400, 400 + n), (DS, 4, 5 * n, 5), ALU.max, f=1.0, n=n)
         ts((pi, a, b), (ti, 0, n), 4095, ALU.bitwise_and)
         if b == P:
             copy((pi, P - 1, P), ("RI%d" % x, P - 1, P))
@@ -281,22 +307,22 @@ def plan(core, T, topo):
     def neck(t, a, b):
         x, y, n = t % 2, cnt[0] % 2, b - a
         NA, OK, PM, pf = "NA%d" % y, "OK%d" % y, "PM%d" % x, "PF%d" % x
-        subtract("SB", ("XP", 16 * a, 16 * b), ("XP", 16 * a + 128, 16 * b + 128))
-        act((NA, 0, 16 * n), ("SB", 0, 16 * n), ACT.Abs)
+        size("SB", ("XP", 16 * a, 16 * b), ("XP", 16 * a + 128, 16 * b + 128), (NA, 0, 16 * n))
         mm(("MS", 0, n), band("Z", NA, 0, n))
         ts((OK, 0, n), ("MS", 0, n), ("THR%d" % t, 0, 1), ALU.is_lt)
         add("v", vc(n), [(OK, 0, n), (PM, 7 + a, 8 + a)], [(PM, 8 + a, 8 + b)],
             lambda e: e.tensor_tensor_scan(T[PM][:, 8 + a:8 + b], T[OK][:, 0:n], T[OK][:, 0:n], T[PM][:, 7 + a:8 + a], ALU.max, ALU.max))
-        mm(("MS", 64, 64 + n), [(("IF", 0, 128), (pf, a + 8, b + 8)), (("IP", 0, 128), ("CN", 0, n)), (("IK", 0, 128), (PM, 7 + a, 7 + b))])
+        mm(("MS", 128, 128 + n), [(("IF", 0, 128), (pf, a + 8, b + 8)), (("IP", 0, 128), ("CN", 0, n)), (("IK", 0, 128), (PM, 7 + a, 7 + b))])
         ti = temp()
-        tt((ti, 0, n), ("MS", 64, 64 + n), (pf, a, b), ALU.max, f=1.0)
+        tt((ti, 0, n), ("MS", 128, 128 + n), (pf, a, b), ALU.max, f=1.0)
         new_r(t, a, b, ti)
 
     def new_r(t, a, b, src):
         x1, n = (t + 1) % 2, b - a
         ts(("RI%d" % x1, a, b), (src, 0, n), 4095, ALU.bitwise_and)
         copy(("RU%d" % x1, a, b), ("RI%d" % x1, a, b))
-        gather(("XR%d" % x1, 16 * a, 16 * b), ("RU%d" % x1, a, b))
+        if not (t == RO - 1 and a >= FUSE):
+            gather(("XR%d" % x1, 16 * a, 16 * b), ("RU%d" % x1, a, b))
         if t < RO - 1:
             from_r(t + 1, a, b)
         else:
@@ -307,12 +333,19 @@ def plan(core, T, topo):
     def border(t, a, b):
         x, x1, y, n = t % 2, (t + 1) % 2, cnt[0] % 2, b - a
         MX, MB = "MX%d" % y, "MB%d" % y
-        subtract("SB", ("XR%d" % x1, 16 * a, 16 * b), ("XM%d" % x, 16 * a, 16 * b))
-        act((MX, 0, 16 * n), ("SB", 0, 16 * n), ACT.Abs)
+        if t == RO - 1 and a >= FUSE:
+            d0, m = SM * (cnt[1] % 4), ("XM%d" % x, 16 * a, 16 * b)
+            cnt[1] += 1
+            off, out = ("RU%d" % x1, a, b), ("XD", d0, d0 + 16 * n)
+            add("v", 0.06 + 16 * n * CYC * GAM, [("FL", 0, W), off, m], [out],
+                lambda e: e.tensor_tensor(ap(out), T.FL[:, 0:W].indirect(ap(off)), ap(m), ALU.subtract))
+            act((MX, 0, 16 * n), out, ACT.Abs)
+        else:
+            size("SB", ("XR%d" % x1, 16 * a, 16 * b), ("XM%d" % x, 16 * a, 16 * b), (MX, 0, 16 * n))
         ts((MB, 0, 16 * n), (MX, 0, 16 * n), ("EPF", 0, 1), ALU.is_gt, f=0.5)
-        mm(("KY", 320, 320 + n), [(("IF", 0, 128), ("RA%d" % x1, 8 + a, 8 + b)), (("IP", 0, 128), ("CP", 0, n))] + band("ZH", MB, 0, n))
+        mm(("KY", 424, 424 + n), [(("IF", 0, 128), ("RA%d" % x1, 8 + a, 8 + b)), (("IP", 0, 128), ("CP", 0, n))] + band("ZH", MB, 0, n))
         ti = temp()
-        tt((ti, 0, n), ("KY", 320, 320 + n), ("MH%d" % x, a, b), ALU.min, f=1.0)
+        tt((ti, 0, n), ("KY", 424, 424 + n), ("MH%d" % x, a, b), ALU.min, f=1.0)
         ts(("MI%d" % x1, a, b), (ti, 0, n), 4095, ALU.bitwise_and)
         if t < RO - 1:
             from_m(t + 1, a, b)
@@ -325,14 +358,12 @@ def plan(core, T, topo):
         add("v", vc(184), [(PM, 8, 192)], [("SPM", 0, 1)],
             lambda e: e.tensor_reduce(T.SPM[:, :], T[PM][:, 8:192], AxisListType.X, ALU.add))
         ts(("OFF", 0, 8), ("K8", 0, 8), ("SPM", 0, 1), ALU.subtract)
-        add("v", 0.3, [("OFF", 0, 8), (pf, 0, 200)], [("LG", 0, 128)],
-            lambda e: e.tensor_copy(T.LG[:, :], T[pf][:, 0:200].indirect(T.OFF[:, 0:8])))
-        tt(("LM", 0, 128), ("LG", 0, 128), ("DM", 0, 128), ALU.mult)
-        src = "LM"
-        for w, dst in ((64, "L64"), (32, "L32"), (16, "L16"), (8, "LO")):
-            tt((dst, 0, w), (src, 0, 2 * w, 2), (src, 1, 2 * w, 2), ALU.add, n=w)
-            src = dst
-        ts(("SND%d" % t, 0, 8), ("LO", 0, 8), 4096.0, ALU.add, (PM, 191, 192), ALU.mult)
+        add("v", 0.06 + 128 * CYC * GAM, [("OFF", 0, 8), (pf, 0, 200), ("DM", 0, 128)], [("LG", 0, 128)],
+            lambda e: e.tensor_tensor(T.LG[:, :], T[pf][:, 0:200].indirect(T.OFF[:, 0:8]), T.DM[:, :], ALU.mult))
+        add("v", vc(128), [("RSL", 0, 128), ("LG", 0, 128)], [("LM", 0, 128)],
+            lambda e: e.tensor_tensor_scan(T.LM[:, :], T.RSL[:, :], T.LG[:, :], 0.0, ALU.mult, ALU.add))
+        own = ("LM", 15, 128, 16)
+        ts(("SND%d" % t, 0, 8), own, 4096.0, ALU.add, (PM, 191, 192), ALU.mult, n=8)
         dst = T.cores[(rank + 1 + t % 3) % len(T.cores)]
         eng = topo.engines(core, dst)[:8]
         msk = 0
@@ -341,12 +372,12 @@ def plan(core, T, topo):
         rid, pid = topo.addr(dst, core)
         send = add("g", 0.5, [("SND%d" % t, 0, 8)], [],
                    lambda e: e.remote_dma(T["LAND%d" % t][:, :], T["SND%d" % t][:, :], T.sem["arr%d" % t], T.sem.sent, pid, rid, msk),
-                   sem="sent", inc=len(eng), free=True)
+                   sem="sent", inc=len(eng))
         src_core = T.cores[(rank - 1 - t % 3) % len(T.cores)]
         add("x", 4.0, [], [("LAND%d" % t, 0, 8)], None, sem="arr%d" % t, inc=len(topo.engines(src_core, core)[:8]), after=[send])
         ts(("NPM", 0, 1), (PM, 191, 192), -1.0, ALU.mult, 1.0, ALU.add)
         ts(("RTK", 0, 8), (pf, 184, 192), 8192.0, ALU.add, ("NPM", 0, 1), ALU.mult)
-        tt(("BASE", 0, 8), ("LO", 0, 8), ("RTK", 0, 8), ALU.max)
+        tt(("BASE", 0, 8), own, ("RTK", 0, 8), ALU.max)
         ts(("THR%d" % (t + 1), 0, 1), (PM, 191, 192), 16.0, ALU.mult, ("THR%d" % t, 0, 1), ALU.add)
 
     def tail(t):
@@ -355,7 +386,7 @@ def plan(core, T, topo):
         new_r(t, 184, 192, ti)
 
     def store(k, out, src):
-        add("y", 2.0, [src], [], lambda e: e.dma_start(out, ap(src)), sem="st%d" % k, inc=16, free=True)
+        add("y", 2.0, [src], [], lambda e: e.dma_start(out, ap(src)), sem="st%d" % k, inc=16)
 
     copy(("RU0", 0, P), ("RI0", 0, P))
     from_r(0, 0, P)
@@ -400,9 +431,7 @@ def depend(ops):
                         continue
                     hit = a < e and c < b
                     if hit and (w or ww):
-                        raw = ww
-                        if raw or j not in d:
-                            d[j] = d.get(j, False) or raw
+                        d[j] = True
         for lst, w in ((o["r"], False), (o["w"], True)):
             for x in lst:
                 n, a, b = x[0], x[1], x[2]
@@ -477,8 +506,7 @@ def schedule(ops, deps):
         for b in banks[k]:
             user.setdefault(b, {})[q] = k
         start[k], qof[k] = s, q
-        issue = 0.06 if ops[k]["q"] in ("y", "sd") else ops[k]["cost"]
-        free[q] = s + issue if q != "x" else 0.0
+        free[q] = s + ops[k]["iss"] if q != "x" else 0.0
         done[k] = s + ops[k]["cost"]
         order.append(k)
         for u in set(users[k]):

import numpy as np
from concourse.mybir import AluOpType as ALU, AxisListType, ActivationFunctionType as ACT

W, P, L, RO = 4096, 192, 8, 3
H = 262144
NM = 96
SM = 16 * NM
CH = [[76, 140, 192], [64, 128, 192], [48, 116, 192]]
BF, F32, I32, U16 = "bfloat16", "float32", "int32", "uint16"

SCRATCH = {
    "FL": ("sbuf", [128, W], BF),
    "ONE": ("sbuf", [128, 144], BF), "Z": ("sbuf", [128, 144], BF), "ZK": ("sbuf", [128, 144], BF), "ZH": ("sbuf", [128, 144], BF),
    "WI": ("sbuf", [128, 144], I32), "WJ": ("sbuf", [128, 5 * NM], I32), "WK": ("sbuf", [128, 128], I32),
    "IP": ("sbuf", [128, 128], BF), "IN": ("sbuf", [128, 128], BF), "IK": ("sbuf", [128, 128], BF), "IF": ("sbuf", [128, 128], F32),
    "KL": ("sbuf", [128, 128], BF), "KR": ("sbuf", [128, 5 * NM], BF), "CP": ("sbuf", [128, NM], BF), "CN": ("sbuf", [128, NM], BF),
    "CC": ("sbuf", [128, 5 * NM], BF), "RSK": ("sbuf", [128, 5 * NM], F32), "RST": ("sbuf", [128, 5 * NM], F32), "DM": ("sbuf", [128, 128], F32), "K8": ("sbuf", [128, 8], F32),
    "thi": ("sbuf", [128, 1], I32), "epi": ("sbuf", [128, 1], I32), "EPF": ("sbuf", [128, 1], F32),
    "OUTR": ("sbuf", [128, P], F32), "OUTM": ("sbuf", [128, P], F32), "OUTA": ("sbuf", [128, 1], F32),
    "LG": ("sbuf", [128, 128], F32), "LM": ("sbuf", [128, 128], F32), "RSL": ("sbuf", [128, 128], F32),
    "SPM": ("sbuf", [128, 1], F32), "OFF": ("sbuf", [128, 8], U16),
    "NPM": ("sbuf", [128, 1], F32), "RTK": ("sbuf", [128, 8], F32), "BASE": ("sbuf", [128, 8], F32),
    "SA": ("psum", [128, 1024], F32), "SB": ("psum", [128, 1024], F32), "KY": ("psum", [128, 512], F32),
    "TB": ("psum", [128, 512], F32), "MS": ("psum", [128, 512], F32), "RV": ("psum", [128, 512], F32),
}
for _m in range(4):
    SCRATCH["IM%d" % _m] = ("sbuf", [128, 128], BF)
for _t in range(RO):
    SCRATCH["SND%d" % _t] = ("sbuf", [128, 8], F32)
    SCRATCH["LAND%d" % _t] = ("sbuf", [128, 8], F32)
for _t in range(RO + 1):
    SCRATCH["THR%d" % _t] = ("sbuf", [128, 1], F32)
for _k in range(2):
    for _n, _w, _d in (("XR", 3088, BF), ("XM", 3072, BF), ("ABS", 5 * SM, BF), ("NOW", SM, BF), ("FB", SM, BF), ("NA", SM, BF),
                       ("MX", SM, BF), ("MB", SM, BF), ("QF", 4 * NM, F32), ("QI", 4 * NM, I32), ("CI", 4 * NM, I32), ("CU", 4 * NM, U16),
                       ("TS", 5 * NM, F32), ("KS", 5 * NM, F32), ("KI", NM, I32), ("KO", NM, I32), ("KU", NM, U16), ("NI", NM, I32),
                       ("NB", NM, BF), ("DS", 5 * NM, F32), ("OK", NM, BF), ("RI", P, I32), ("RU", P, U16), ("RA", 208, F32),
                       ("MI", P, I32), ("MU", P, U16), ("MA", 208, F32), ("MH", P, F32), ("PI", P, I32), ("PU", P, U16),
                       ("PF", 200, F32), ("PM", 208, BF)):
        SCRATCH["%s%d" % (_n, _k)] = ("sbuf", [128, _w], _d)
SCRATCH["XP"] = ("sbuf", [128, 3072], BF)
SCRATCH["XD"] = ("sbuf", [128, 4 * SM], BF)

for _k in range(4):
    SCRATCH["TI%d" % _k] = ("sbuf", [128, NM], I32)
QSEM = {"v": "cv", "s": "cs", "t": "ct", "g": "cg"}
SEMAPHORES = ["cv", "cs", "ct", "cg", "sent", "arr0", "arr1", "arr2"] + ["ld%d" % k for k in range(6)] + ["st%d" % k for k in range(8)] + ["ac%d" % k for k in range(32)]
CYC = 0.83e-3 * 1.25
GAM = 1.5
WAKE = 0.08
SLACK, NOISE, SEED = 0.0, 0.003, 991
PLAIN = [(), (0,), (1,), (0,), (3,), (), (1,), (), (3,), (1,)]
PEF = 0.5
AGE = 0.0
UNIT = 512
FUSE = 40
GQ = [{"x": "vs"}.get(c, c) for c in "ssxvsssxsssvssxsssvssxssxsxxxxsxssxsvssvvsvvssvv"]


def plan(core, T, topo):
    ops = []
    rank = T.rank_of(core)

    def add(q, cost, reads, writes, fn, sem=None, inc=1, after=(), iss=None):
        if iss is None:
            iss = 0.06 if q in ("y", "sd") else cost
        ops.append({"q": q, "cost": cost, "r": reads, "w": writes, "fn": fn, "sem": sem, "inc": inc, "after": list(after),
                    "iss": iss})
        return len(ops) - 1

    def ap(x):
        n, a, b = x[0], x[1], x[2]
        return T[n][:, a:b] if len(x) == 3 else T[n][:, a:b:x[3]]

    def vc(n, f=1.0):
        return max(64, n * f) * CYC + 0.02

    def copy(out, in_, f=1.0):
        add("v", vc((out[2] - out[1]) // (out[3] if len(out) > 3 else 1), f), [in_], [out], lambda e: e.tensor_copy(ap(out), ap(in_)))

    def ts(out, in_, s1, op0, s2=None, op1=None, f=1.0, n=None):
        rd = [in_] + [s for s in (s1, s2) if not isinstance(s, (int, float)) and s is not None]
        v1 = s1 if isinstance(s1, (int, float)) else ap(s1)
        v2 = s2 if s2 is None or isinstance(s2, (int, float)) else ap(s2)
        if op1 is None:
            add("v", vc(n or in_[2] - in_[1], f), rd, [out], lambda e: e.tensor_scalar(ap(out), ap(in_), v1, None, op0))
        else:
            add("v", vc(n or in_[2] - in_[1], f), rd, [out], lambda e: e.tensor_scalar(ap(out), ap(in_), v1, v2, op0, op1))

    def scaled(out, in_, c):
        def fn(e, qn):
            if qn == "v":
                return e.tensor_scalar(ap(out), ap(in_), c, None, ALU.mult)
            return e.activation(ap(out), ap(in_), ACT.Copy, 0.0, c)
        add("vs", vc(out[2] - out[1]), [in_], [out], fn)

    def tt(out, a, b, op, f=2.0, n=None):
        add("v", vc(n or b[2] - b[1], f), [a, b], [out], lambda e: e.tensor_tensor(ap(out), ap(a), ap(b), op))

    def memset(x, c):
        add("v", vc(x[2] - x[1]), [], [x], lambda e: e.memset(ap(x), c))

    def act(out, in_, func):
        add("s", 0.065 + (in_[2] - in_[1]) * CYC, [in_], [out], lambda e: e.activation(ap(out), ap(in_), func))

    gn = [0]

    def gather(out, off):
        q = GQ[gn[0] % len(GQ)]
        gn[0] += 1

        def fn(e, qn):
            src = T.FL[:, 0:W].indirect(ap(off))
            return e.tensor_copy(ap(out), src) if qn == "v" else e.activation(ap(out), src, ACT.Copy)
        add(q, 0.06 + (out[2] - out[1]) * CYC * GAM, [("FL", 0, W), off], [out], lambda e: fn(e, "v" if q == "v" else "s"))
        if len(q) == 2:
            ops[-1]["fn"] = fn

    def mm(out, terms):
        def fn(e):
            ins = None
            for k, (l, r) in enumerate(terms):
                ins = e.matmul(ap(out), ap(l), ap(r), k == 0, k == len(terms) - 1)
            return ins
        cost = 0.0
        for l, r in terms:
            n = (r[2] - r[1] + (r[3] if len(r) > 3 else 1) - 1) // (r[3] if len(r) > 3 else 1)
            cost += max(64, n) * (4 if l[0] == "IF" else 1) * PEF * CYC
        hull = {}
        for x in [x for l, r in terms for x in (l, r)]:
            c, d = hull.get(x[0], (x[1], x[2]))
            hull[x[0]] = (min(c, x[1]), max(d, x[2]))
        add("t", cost + 0.03, [(h, hull[h][0], hull[h][1]) for h in sorted(hull)], [out], fn)

    def band(z, src, c0, n):
        return [((z, 15 - p, 143 - p), (src, c0 + p, c0 + 16 * n, 16)) for p in range(16)]

    def subtract(slot, a, b):
        n = a[2] - a[1]
        for c in range(0, n, 512):
            d = min(n, c + 512)
            mm((slot, c, d), [(("IP", 0, 128), (a[0], a[1] + c, a[1] + d)), (("IN", 0, 128), (b[0], b[1] + c, b[1] + d))])

    turn = [0]

    def size(slot, a, b, out):
        n = a[2] - a[1]
        if n <= UNIT:
            subtract(slot, a, b)
            act(out, (slot, 0, n), ACT.Abs)
            return
        h = (n // -(-n // 512) + 15) // 16 * 16
        for c in range(0, n, h):
            d = min(n, c + h)
            o = 512 * (turn[0] % 2)
            turn[0] += 1
            mm((slot, o, o + d - c), [(("IP", 0, 128), (a[0], a[1] + c, a[1] + d)), (("IN", 0, 128), (b[0], b[1] + c, b[1] + d))])
            act((out[0], out[1] + c, out[1] + d), (slot, o, o + d - c), ACT.Abs)

    def load(q, k, out, src):
        add(q, 2.0 if k != 5 else 6.0, [], [out], lambda e: e.dma_start(ap(out), src), sem="ld%d" % k, inc=16)
    load("y", 0, ("RI0", 0, P), T.riv[:, :])
    load("sd", 1, ("MI0", 0, P), T.bord[:, :])
    load("y", 5, ("FL", 0, W), T.flood[:, :])
    load("sd", 2, ("thi", 0, 1), T.th[:, :])
    load("sd", 3, ("epi", 0, 1), T.eps[:, :])

    memset(("ONE", 0, 144), 1.0)
    add("g", 0.5, [], [("WI", 0, 144)], lambda e: e.iota(T.WI[:, :], [[1, 144]], 1, 0))
    add("g", 0.5, [("ONE", 0, 128)], [("IP", 0, 128)],
        lambda e: e.affine_select(T.IP[:, :], T.ONE[:, 0:128], [[-1, 128]], ALU.is_equal, 0.0, 0, 1))
    ts(("WI", 0, 144), ("WI", 0, 144), 15, ALU.bitwise_and)
    ts(("Z", 0, 144), ("WI", 0, 144), 0.0, ALU.is_equal)
    add("g", 0.5, [("Z", 0, 144)], [("Z", 0, 144)],
        lambda e: e.affine_select(T.Z[:, :], T.Z[:, :], [[-1, 144]], ALU.is_ge, 0.0, 15, 1))
    add("g", 0.5, [("Z", 0, 144)], [("Z", 0, 144)],
        lambda e: e.affine_select(T.Z[:, :], T.Z[:, :], [[1, 144]], ALU.is_ge, 0.0, 0, -1))
    add("g", 1.0, [], [("WJ", 0, 5 * NM)], lambda e: e.iota(T.WJ[:, :], [[0, NM], [1, 5]], 0, 0))
    ts(("RST", 0, 5 * NM), ("WJ", 0, 5 * NM), 0.0, ALU.is_equal)
    ts(("RSK", 0, 5 * NM), ("RST", 0, 5 * NM), 67108864.0, ALU.mult, -33554432.0, ALU.add)
    scaled(("RST", 0, 5 * NM), ("RSK", 0, 5 * NM), -1.0)
    scaled(("IF", 0, 128), ("IP", 0, 128), 1.0)
    scaled(("IN", 0, 128), ("IP", 0, 128), -1.0)
    scaled(("IK", 0, 128), ("IP", 0, 128), 8192.0)
    for m in range(4):
        scaled(("IM%d" % m, 0, 128), ("IP", 0, 128), 8192.0 * (m - 4))
    scaled(("ZK", 0, 144), ("Z", 0, 144), 8192.0)
    scaled(("ZH", 0, 144), ("Z", 0, 144), float(H))
    memset(("CP", 0, NM), 2048.0)
    memset(("CN", 0, NM), -4096.0)
    for m in range(4):
        memset(("CC", NM * m, NM * m + NM), -4096.0 * (m - 4) ** 2)
    memset(("CC", 4 * NM, 5 * NM), -7.5 * H)
    memset(("KL", 0, 128), 0.0)
    memset(("KR", 0, 5 * NM), 0.0)

    def row(name, part, n, c):
        add("v", vc(n), [], [(name, 0, n)], lambda e: e.memset(T[name][part:part + 1, 0:n], c))

    def irow(name, part, n, pat):
        add("g", 0.6, [], [(name, 0, n)],
            lambda e: e.iota(T[name][part:part + 1, 0:n], pat, 0, 0, allow_small_or_imprecise_dtypes=True))
    row("KL", 0, 128, 1.0)
    row("KL", 32, 128, 1.0)
    row("KL", 96, 128, 1.0)
    row("KR", 64, 5 * NM, 1.0)
    row("KR", 96, 5 * NM, -16777216.0)
    irow("KL", 64, 128, [[0, 8], [1, 16]])
    irow("KR", 0, 5 * NM, [[SM, 5], [0, NM]])
    irow("KR", 32, 5 * NM, [[0, 5], [16, NM]])
    add("g", 0.5, [], [("WK", 0, 128)], lambda e: e.iota(T.WK[:, :], [[1, 128]], 128, -1))
    ts(("WK", 0, 128), ("WK", 0, 128), 15, ALU.bitwise_and)
    ts(("DM", 0, 128), ("WK", 0, 128), 0.0, ALU.is_equal)
    ts(("RSL", 0, 128), ("WI", 15, 143), 0.0, ALU.not_equal)
    add("g", 0.2, [], [("K8", 0, 8)], lambda e: e.iota(T.K8[:, :], [[1, 8]], 185, 0, allow_small_or_imprecise_dtypes=True))
    for k in range(2):
        memset(("RA%d" % k, 200, 208), 0.0)
        memset(("MA%d" % k, 192, 208), 0.0)
        memset(("XR%d" % k, 3072, 3088), 0.0)
        memset(("PF%d" % k, 192, 200), 0.0)
        memset(("PM%d" % k, 0, 8), 0.0)
    copy(("THR0", 0, 1), ("thi", 0, 1))
    copy(("EPF", 0, 1), ("epi", 0, 1))

    def from_r(t, a, b):
        x = t % 2
        ts(("RA%d" % x, 8 + a, 8 + b), ("RI%d" % x, a, b), 2048.0, ALU.subtract)
        if a == 0:
            ts(("RA%d" % x, 7, 8), ("RI%d" % x, 0, 1), 2048.0, ALU.subtract)
        ts(("RV", a, b), ("RI%d" % x, a, b), 32.0, ALU.add)
        ts(("RV", 192 + a, 192 + b), ("RI%d" % x, a, b), 3232.0, ALU.mult, float(65536 + 2464 * t - 8388608), ALU.add)

    def from_m(t, a, b):
        x = t % 2
        copy(("MU%d" % x, a, b), ("MI%d" % x, a, b))
        ts(("MA%d" % x, a, b), ("MI%d" % x, a, b), 2048.0, ALU.subtract)
        ts(("MH%d" % x, a, b), ("MI%d" % x, a, b), 7.5 * H, ALU.add)

    cnt = [0, 0, 0, 0]

    def temp():
        cnt[2] += 1
        return "TI%d" % (cnt[2] % 4)

    def step1(t, a, b):
        x, y = t % 2, cnt[0] % 2
        cnt[0] += 1
        n = b - a
        N = ("XR%d" % x, 16 * (a + 1), 16 * (b + 1))
        QF, QI, CI, CU, TS = ("%s%d" % (s, y) for s in ("QF", "QI", "CI", "CU", "TS"))
        ABS, NOW, FB, KS, DS = ("%s%d" % (s, y) for s in ("ABS", "NOW", "FB", "KS", "DS"))
        KI, KO, KU, NI, NB = ("%s%d" % (s, y) for s in ("KI", "KO", "KU", "NI", "NB"))
        ra, ma = "RA%d" % x, "MA%d" % x
        for m, (nm, o) in enumerate(((ra, 7 + a), (ra, 9 + a), (ma, a), (ma, a + 1))):
            tt((QF, m * n, m * n + n), (nm, o, o + n), ("RV", a, b), ALU.mult, f=1.0)
        for m in range(4):
            tt((QI, m * n, m * n + n), (QF, m * n, m * n + n), ("RV", 192 + a, 192 + b), ALU.add, f=1.0)
        for h in (0, 2 * n):
            ts((CI, h, h + 2 * n), (QI, h, h + 2 * n), 5, ALU.arith_shift_right, 4095, ALU.bitwise_and)
            copy((CU, h, h + 2 * n), (CI, h, h + 2 * n))
        size("SA", ("XR%d" % x, 16 * a, 16 * b), N, (NOW, 0, 16 * n))
        size("SA", ("XM%d" % x, 16 * a, 16 * b), N, (ABS, 4 * SM, 4 * SM + 16 * n))
        for m in range(4):
            d0 = SM * (cnt[1] % 4)
            cnt[1] += 1
            off, out = (CU, m * n, m * n + n), ("XD", d0, d0 + 16 * n)
            if m in PLAIN[(cnt[0] - 1) % len(PLAIN)]:
                add("s", 0.065 + 16 * n * CYC * GAM, [("FL", 0, W), off], [out],
                    lambda e, o=out, f=off: e.activation(ap(o), T.FL[:, 0:W].indirect(ap(f)), ACT.Copy, 0.0, -1.0))
                add("g", 3.5, [out, N], [out], lambda e, o=out: e.dma_start(ap(o), ap(N), accum_op=ALU.add),
                    sem="ac%d" % cnt[3], inc=16, iss=1.1)
                cnt[3] += 1
                act((ABS, SM * m, SM * m + 16 * n), out, ACT.Abs)
                continue
            add("v", 0.06 + 16 * n * CYC * GAM, [("FL", 0, W), off, N], [out],
                lambda e, o=out, f=off: e.tensor_tensor(ap(o), T.FL[:, 0:W].indirect(ap(f)), ap(N), ALU.subtract))
            act((ABS, SM * m, SM * m + 16 * n), out, ACT.Abs)
        for m in (4, 0, 1, 2, 3):
            mm(("KY", m, 5 * n, 5), [(("KL", 0, 128), ("KR", NM * m, NM * m + n))] + band("ZK", ABS, SM * m, n))
        add("v", vc(5 * n), [("RSK", 0, 5 * n), ("KY", 0, 5 * n)], [(KS, 0, 5 * n)],
            lambda e: e.tensor_tensor_scan(T[KS][:, 0:5 * n], T.RSK[:, 0:5 * n], T.KY[:, 0:5 * n], 0.0, ALU.max, ALU.min))
        copy((KI, 0, n), (KS, 4, 5 * n, 5), f=1.0)
        ts((KO, 0, n), (KI, 0, n), 8191, ALU.bitwise_and)
        copy((KU, 0, n), (KO, 0, n))
        ts((NI, 0, n), (KO, 0, n), 1.0 / SM, ALU.mult, -0.4995, ALU.add)
        ts((NB, 0, n), (NI, 0, n), 4.0, ALU.subtract)
        add("v", 0.06 + 16 * n * CYC * GAM, [(ABS, 0, 4 * SM + 16 * n), (KU, 0, n), (NOW, 0, 16 * n)], [(FB, 0, 16 * n)],
            lambda e: e.tensor_tensor(T[FB][:, 0:16 * n], T[ABS][:, 0:4 * SM + 16 * n].indirect(T[KU][:, 0:n]), T[NOW][:, 0:16 * n], ALU.is_ge))
        for m in range(4):
            mm(("TB", m * n, m * n + n), [(("IP", 0, 128), ("CC", NM * m, NM * m + n)), (("IM%d" % m, 0, 128), (NB, 0, n))])
            tt((TS, m, 5 * n, 5), ("TB", m * n, m * n + n), (CI, m * n, m * n + n), ALU.add, f=1.0)
        copy((TS, 4, 5 * n, 5), ("MI%d" % x, a, b))
        add("v", vc(5 * n), [("RST", 0, 5 * n), (TS, 0, 5 * n)], [(DS, 0, 5 * n)],
            lambda e: e.tensor_tensor_scan(T[DS][:, 0:5 * n], T.RST[:, 0:5 * n], T[TS][:, 0:5 * n], 0.0, ALU.min, ALU.max))
        mm(("TB", 400, 400 + n), [(("IF", 0, 128), (ra, 8 + a, 8 + b)), (("IP", 0, 128), ("CP", 0, n)),
                                  (("IP", 0, 128), ("CC", 4 * NM, 4 * NM + n))]
           + band("ZH", FB, 0, n))
        pi, ti = "PI%d" % x, temp()
        tt((ti, 0, n), ("TB", 400, 400 + n), (DS, 4, 5 * n, 5), ALU.max, f=1.0, n=n)
        ts((pi, a, b), (ti, 0, n), 4095, ALU.bitwise_and)
        if b == P:
            copy((pi, P - 1, P), ("RI%d" % x, P - 1, P))
        copy(("PU%d" % x, a, b), (pi, a, b))
        copy(("PF%d" % x, a, b), (pi, a, b))
        gather(("XP", 16 * a, 16 * b), ("PU%d" % x, a, b))

    def neck(t, a, b):
        x, y, n = t % 2, cnt[0] % 2, b - a
        NA, OK, PM, pf = "NA%d" % y, "OK%d" % y, "PM%d" % x, "PF%d" % x
        size("SB", ("XP", 16 * a, 16 * b), ("XP", 16 * a + 128, 16 * b + 128), (NA, 0, 16 * n))
        mm(("MS", 0, n), band("Z", NA, 0, n))
        ts((OK, 0, n), ("MS", 0, n), ("THR%d" % t, 0, 1), ALU.is_lt)
        add("v", vc(n), [(OK, 0, n), (PM, 7 + a, 8 + a)], [(PM, 8 + a, 8 + b)],
            lambda e: e.tensor_tensor_scan(T[PM][:, 8 + a:8 + b], T[OK][:, 0:n], T[OK][:, 0:n], T[PM][:, 7 + a:8 + a], ALU.max, ALU.max))
        mm(("MS", 128, 128 + n), [(("IF", 0, 128), (pf, a + 8, b + 8)), (("IP", 0, 128), ("CN", 0, n)), (("IK", 0, 128), (PM, 7 + a, 7 + b))])
        ti = temp()
        tt((ti, 0, n), ("MS", 128, 128 + n), (pf, a, b), ALU.max, f=1.0)
        new_r(t, a, b, ti)

    def new_r(t, a, b, src):
        x1, n = (t + 1) % 2, b - a
        ts(("RI%d" % x1, a, b), (src, 0, n), 4095, ALU.bitwise_and)
        copy(("RU%d" % x1, a, b), ("RI%d" % x1, a, b))
        if not (t == RO - 1 and a >= FUSE):
            gather(("XR%d" % x1, 16 * a, 16 * b), ("RU%d" % x1, a, b))
        if t < RO - 1:
            from_r(t + 1, a, b)
        else:
            copy(("OUTR", a, b), ("RI%d" % x1, a, b))
            ts(("RA%d" % x1, 8 + a, 8 + b), ("RI%d" % x1, a, b), 2048.0, ALU.subtract)
        border(t, a, b)

    def border(t, a, b):
        x, x1, y, n = t % 2, (t + 1) % 2, cnt[0] % 2, b - a
        MX, MB = "MX%d" % y, "MB%d" % y
        if t == RO - 1 and a >= FUSE:
            d0, m = SM * (cnt[1] % 4), ("XM%d" % x, 16 * a, 16 * b)
            cnt[1] += 1
            off, out = ("RU%d" % x1, a, b), ("XD", d0, d0 + 16 * n)
            add("v", 0.06 + 16 * n * CYC * GAM, [("FL", 0, W), off, m], [out],
                lambda e: e.tensor_tensor(ap(out), T.FL[:, 0:W].indirect(ap(off)), ap(m), ALU.subtract))
            act((MX, 0, 16 * n), out, ACT.Abs)
        else:
            size("SB", ("XR%d" % x1, 16 * a, 16 * b), ("XM%d" % x, 16 * a, 16 * b), (MX, 0, 16 * n))
        ts((MB, 0, 16 * n), (MX, 0, 16 * n), ("EPF", 0, 1), ALU.is_gt, f=0.5)
        mm(("KY", 424, 424 + n), [(("IF", 0, 128), ("RA%d" % x1, 8 + a, 8 + b)), (("IP", 0, 128), ("CP", 0, n))] + band("ZH", MB, 0, n))
        ti = temp()
        tt((ti, 0, n), ("KY", 424, 424 + n), ("MH%d" % x, a, b), ALU.min, f=1.0)
        ts(("MI%d" % x1, a, b), (ti, 0, n), 4095, ALU.bitwise_and)
        if t < RO - 1:
            from_m(t + 1, a, b)
            gather(("XM%d" % x1, 16 * a, 16 * b), ("MU%d" % x1, a, b))
        else:
            copy(("OUTM", a, b), ("MI%d" % x1, a, b))

    def loops(t):
        x, PM, pf = t % 2, "PM%d" % (t % 2), "PF%d" % (t % 2)
        add("v", vc(184), [(PM, 8, 192)], [("SPM", 0, 1)],
            lambda e: e.tensor_reduce(T.SPM[:, :], T[PM][:, 8:192], AxisListType.X, ALU.add))
        ts(("OFF", 0, 8), ("K8", 0, 8), ("SPM", 0, 1), ALU.subtract)
        add("v", 0.06 + 128 * CYC * GAM, [("OFF", 0, 8), (pf, 0, 200), ("DM", 0, 128)], [("LG", 0, 128)],
            lambda e: e.tensor_tensor(T.LG[:, :], T[pf][:, 0:200].indirect(T.OFF[:, 0:8]), T.DM[:, :], ALU.mult))
        add("v", vc(128), [("RSL", 0, 128), ("LG", 0, 128)], [("LM", 0, 128)],
            lambda e: e.tensor_tensor_scan(T.LM[:, :], T.RSL[:, :], T.LG[:, :], 0.0, ALU.mult, ALU.add))
        own = ("LM", 15, 128, 16)
        ts(("SND%d" % t, 0, 8), own, 4096.0, ALU.add, (PM, 191, 192), ALU.mult, n=8)
        dst = T.cores[(rank + 1 + t % 3) % len(T.cores)]
        eng = topo.engines(core, dst)[:8]
        msk = 0
        for q in eng:
            msk |= 1 << q
        rid, pid = topo.addr(dst, core)
        send = add("g", 0.5, [("SND%d" % t, 0, 8)], [],
                   lambda e: e.remote_dma(T["LAND%d" % t][:, :], T["SND%d" % t][:, :], T.sem["arr%d" % t], T.sem.sent, pid, rid, msk),
                   sem="sent", inc=len(eng))
        src_core = T.cores[(rank - 1 - t % 3) % len(T.cores)]
        add("x", 4.0, [], [("LAND%d" % t, 0, 8)], None, sem="arr%d" % t, inc=len(topo.engines(src_core, core)[:8]), after=[send])
        ts(("NPM", 0, 1), (PM, 191, 192), -1.0, ALU.mult, 1.0, ALU.add)
        ts(("RTK", 0, 8), (pf, 184, 192), 8192.0, ALU.add, ("NPM", 0, 1), ALU.mult)
        tt(("BASE", 0, 8), own, ("RTK", 0, 8), ALU.max)
        ts(("THR%d" % (t + 1), 0, 1), (PM, 191, 192), 16.0, ALU.mult, ("THR%d" % t, 0, 1), ALU.add)

    def tail(t):
        ti = temp()
        tt((ti, 0, 8), ("BASE", 0, 8), ("LAND%d" % t, 0, 8), ALU.max)
        new_r(t, 184, 192, ti)

    def store(k, out, src):
        add("y", 2.0, [src], [], lambda e: e.dma_start(out, ap(src)), sem="st%d" % k, inc=16)

    copy(("RU0", 0, P), ("RI0", 0, P))
    from_r(0, 0, P)
    from_m(0, 0, P)
    bs = CH[0]
    for a, b in zip([0] + bs[:-1], bs):
        gather(("XR0", 16 * a, 16 * b), ("RU0", a, b))
        gather(("XM0", 16 * a, 16 * b), ("MU0", a, b))
    chunks = [(t, a, b) for t in range(RO) for a, b in zip([0] + CH[t][:-1], CH[t])]

    def rest(c):
        t, a, b = c
        neck(t, max(a - 8, 0), b - 8)
        if b == P:
            loops(t)
            if t == RO - 1:
                store(0, T.yr[:, 0:184], ("OUTR", 0, 184))
                store(1, T.ym[:, 0:184], ("OUTM", 0, 184))
                ts(("OUTA", 0, 1), ("THR3", 0, 1), ("THR0", 0, 1), ALU.subtract, 0.0625, ALU.mult)
                store(2, T.ya[:, :], ("OUTA", 0, 1))
            tail(t)
    for k, c in enumerate(chunks):
        step1(*c)
        if k:
            rest(chunks[k - 1])
    rest(chunks[-1])
    store(3, T.yr[:, 184:192], ("OUTR", 184, 192))
    store(4, T.ym[:, 184:192], ("OUTM", 184, 192))
    return ops


def depend(ops):
    hist = {}
    deps = []
    for k, o in enumerate(ops):
        d = {}
        for lst, w in ((o["r"], False), (o["w"], True)):
            for x in lst:
                n, a, b = x[0], x[1], x[2]
                for (j, c, e, ww) in hist.get(n, ()):
                    if j == k:
                        continue
                    hit = a < e and c < b
                    if hit and (w or ww):
                        d[j] = True
        for lst, w in ((o["r"], False), (o["w"], True)):
            for x in lst:
                n, a, b = x[0], x[1], x[2]
                h = hist.setdefault(n, [])
                if w and len(x) == 3 and SCRATCH[n][0] != "psum":
                    h[:] = [z for z in h if z[0] == k or not (a <= z[1] and z[2] <= b)]
                h.append((k, a, b, w))
        deps.append(d)
    return deps


def schedule(ops, deps):
    n = len(ops)
    users = [[] for _ in range(n)]
    for k, d in enumerate(deps):
        for j in d:
            users[j].append(k)
        for j in ops[k]["after"]:
            users[j].append(k)
    rank = [0.0] * n
    for k in range(n - 1, -1, -1):
        rank[k] = ops[k]["cost"] + max([rank[u] + WAKE for u in users[k]], default=0.0)
    left = [len(set(list(deps[k]) + ops[k]["after"])) for k in range(n)]
    done, start, qof = [None] * n, [None] * n, [None] * n
    ready = [k for k in range(n) if left[k] == 0]
    rt = [0.0] * n
    free = {q: 0.0 for q in ("v", "s", "t", "g", "y", "x")}
    order = []
    lats = {}
    banks = [sorted({(x[0], c) for x in o["r"] + o["w"] if SCRATCH[x[0]][0] == "psum"
                     for c in range(x[1] // 512, (x[2] - 1) // 512 + 1)}) for o in ops]
    user = {}

    def held(k, q):
        return [j for b in banks[k] for p, j in user.get(b, {}).items() if p != q]

    def latest(k, q):
        lat = 0.0
        for j in deps[k]:
            if qof[j] != q:
                lat = max(lat, done[j] + WAKE)
            elif deps[k][j]:
                lat = max(lat, done[j] + WAKE * 0.6)
        for j in ops[k]["after"]:
            lat = max(lat, done[j])
        return lat
    rng = np.random.RandomState(SEED)
    rank = [r - AGE * k for k, r in enumerate(rank)]
    if NOISE:
        rank = [r + 100 * NOISE * float(z) for r, z in zip(rank, rng.randn(n))]
    while ready:
        best = None
        for q in free:
            cand = []
            for k in ready:
                if q in ("s" if ops[k]["q"] == "sd" else ops[k]["q"]):
                    if (k, q) not in lats:
                        lats[k, q] = latest(k, q)
                    s = max(free[q], lats[k, q])
                    if banks[k]:
                        s = max([s] + [done[j] + WAKE for j in held(k, q)])
                    cand.append((s, k))
            if cand:
                lim = min(cand)[0] + SLACK
                s, k = max(((rank[k], s, k) for s, k in cand if s <= lim))[1:]
                if best is None or s < best[0]:
                    best = (s, k, q)
        s, k, q = best
        ready.remove(k)
        for j in held(k, q):
            deps[k].setdefault(j, False)
        for b in banks[k]:
            user.setdefault(b, {})[q] = k
        start[k], qof[k] = s, q
        free[q] = s + ops[k]["iss"] if q != "x" else 0.0
        done[k] = s + ops[k]["cost"]
        order.append(k)
        for u in set(users[k]):
            left[u] -= 1
            if left[u] == 0:
                ready.append(u)
    return order, qof, start, done


def rank_program(g, core, T, topo):
    if T.rank_of(core) is None:
        return
    ops = plan(core, T, topo)
    deps = depend(ops)
    order, qof, start, done = schedule(ops, deps)
    eng = {"v": g.vector, "s": g.scalar, "t": g.tensor, "g": g, "y": g.sync}
    total, mark, clock, pool = {}, {}, {}, []
    known = {q: {} for q in eng}
    for k in order:
        o, q = ops[k], qof[k]
        sem = o["sem"] or QSEM[q]
        need = {}
        if q == "x":
            total[sem] = total.get(sem, 0) + o["inc"]
            mark[k] = (sem, total[sem])
            clock[k] = {sem: total[sem]}
            continue
        for j in deps[k]:
            if qof[j] == q and (q == "t" or not deps[k][j]) and ops[j]["sem"] is None:
                continue
            s, v = mark[j]
            if known[q].get(s, 0) < v:
                if need.get(s, (0, 0))[0] < v:
                    need[s] = (v, j)
        if q == "g" and o["sem"] is None and pool:
            s, v = mark[pool[-1]]
            if known[q].get(s, 0) < v:
                need[s] = (v, pool[-1])
        if q == "g" and o["sem"] is None:
            pool.append(k)
        for s in sorted(need):
            v, j = need[s]
            if any(s2 != s and clock[need[s2][1]].get(s, 0) >= v for s2 in need):
                continue
            eng[q].wait_ge(T.sem[s], v)
        for s in need:
            v, j = need[s]
            for s2, v2 in clock[j].items():
                known[q][s2] = max(known[q].get(s2, 0), v2)
        ins = o["fn"](eng[q], q) if o["q"] == "vs" else o["fn"](eng[q])
        total[sem] = total.get(sem, 0) + o["inc"]
        mark[k] = (sem, total[sem])
        clock[k] = dict(known[q])
        clock[k][sem] = total[sem]
        if sem != "sent":
            ins.then_inc(T.sem[sem], o["inc"])
    for s in sorted(total):
        if known["y"].get(s, 0) < total[s]:
            g.sync.wait_ge(T.sem[s], total[s])
